import numpy as np
import ml_dtypes


def mxq(x, axis, fmt="e4m3"):
    dtype, down = {"e4m3": (ml_dtypes.float8_e4m3fn, 7), "e5m2": (ml_dtypes.float8_e5m2, 14)}[fmt]
    v = np.moveaxis(np.asarray(x, np.float32).astype(ml_dtypes.bfloat16).astype(np.float64), axis, -1)
    blocks = v.reshape(v.shape[:-1] + (-1, 32))
    amax = np.abs(blocks).max(-1, keepdims=True)
    byte = np.maximum(np.where(amax > 0, np.frexp(amax)[1] - 1 + 127, 0) - down, 1)
    scale = np.exp2(byte - 127.0)
    codes = (blocks / scale).astype(np.float32).astype(dtype).astype(np.float64)
    return np.moveaxis((codes * scale).reshape(v.shape), -1, axis)


WIDE = False


def mx_kscale(k):
    if not WIDE:
        return np.ones(k)
    levels = np.array([10, -10, 5, -5, 0])
    if k % 512:
        return np.exp2(np.random.permutation(np.resize(levels, k // 32))).repeat(32)
    a = np.empty((k // 512, 16))
    for p in range(k // 512):
        a[p, :8] = np.random.permutation(np.resize(levels, 8))
        for g in range(8):
            far = levels[np.abs(levels - a[p, g]) >= 10]
            a[p, g + 8] = far[np.random.randint(len(far))]
    return np.exp2(a.ravel()).repeat(32)


def f64(x):
    return np.asarray(x).astype(np.float64)


def striped(idx):
    return np.tile(idx.reshape(-1, 16).T, (8, 1)).astype(np.uint16)


def unstriped(offs):
    return offs[:16].T.reshape(-1).astype(np.int64)


E2M1 = np.array([0.0, 0.5, 1.0, 1.5, 2.0, 3.0, 4.0, 6.0, -0.0, -0.5, -1.0, -1.5, -2.0, -3.0, -4.0, -6.0])


def pack_weight(w, fmt):
    k, n = w.shape
    w = f64(np.asarray(w, np.float32).astype(ml_dtypes.bfloat16)).reshape(k // 32, 32, n)
    amax = np.abs(w).max(1)
    if fmt == "e4m3":
        byte = np.frexp(amax)[1] - 1 + 127 - 7
    else:
        mant, ex = np.frexp(amax / 6.0)
        byte = np.where(mant > 0.5, ex, ex - 1) + 127
    byte = np.clip(np.where(amax > 0, byte, 1), 1, 254)
    scaled = (w * np.exp2(127.0 - byte)[:, None, :]).reshape(k, n).astype(np.float32)
    by_word = np.ascontiguousarray(scaled.reshape(k // 512, 128, 4, n).transpose(0, 1, 3, 2))
    if fmt == "e4m3":
        words = by_word.astype(ml_dtypes.float8_e4m3fn).view(np.uint8)
    else:
        c = by_word.astype(ml_dtypes.float4_e2m1fn).view(np.uint8) & 0xF
        words = (c[..., 0::2] | (c[..., 1::2] << 4)).reshape(k // 512, 128, 2 * n)
    return np.ascontiguousarray(words), np.ascontiguousarray(byte.astype(np.uint8).reshape(k // 512, 16, n))


def unpack_weight(words, scales, fmt):
    g, _, n = scales.shape
    words = np.ascontiguousarray(words).reshape(g, 128, n, -1)
    if fmt == "e4m3":
        vals = words.view(ml_dtypes.float8_e4m3fn).astype(np.float64)
    else:
        nib = np.empty((g, 128, n, 4), np.uint8)
        nib[..., 0::2] = words & 0xF
        nib[..., 1::2] = words >> 4
        vals = E2M1[nib]
    vals = vals * np.repeat(np.exp2(scales.astype(np.float64) - 127.0), 8, axis=1)[..., None]
    return vals.transpose(0, 1, 3, 2).reshape(g * 512, n)


def gelu(v):
    return 0.5 * v * (1.0 + np.tanh(np.sqrt(2.0 / np.pi) * (v + 0.044715 * v**3)))


K, T, E, C, H, N = 1536, 640, 2, 256, 1024, 384


def by_expert(wq, xq):
    return np.concatenate([wq[e].T @ xq[:, e * C:(e + 1) * C] for e in range(E)], axis=1)


def setup_inputs():
    n = np.random.standard_normal
    s = mx_kscale(K)[:, None]
    u = mx_kscale(H)
    w1 = [pack_weight(m, "e2m1") for m in n((E, K, H)) / np.sqrt(K) / s[None] * u[None, None, :]]
    w2 = [pack_weight(m, "e2m1") for m in n((E, H, N)) / np.sqrt(H) / u[None, :, None]]
    return {
        "xT": (n((K, T)) * s).astype(np.float32),
        "xr": n((N, T)).astype(np.float32),
        "w1_words": np.stack([m[0] for m in w1]),
        "w1_scales": np.stack([m[1] for m in w1]),
        "w2_words": np.stack([m[0] for m in w2]),
        "w2_scales": np.stack([m[1] for m in w2]),
        "gate": np.tile(np.random.uniform(0.2, 1.0, E * C), (N, 1)).astype(np.float32),
        "offs": striped(np.random.permutation(T)[:E * C]),
    }


def reference(xT, xr, w1_words, w1_scales, w2_words, w2_scales, gate, offs):
    idx = unstriped(offs)
    w1 = np.stack([unpack_weight(w1_words[e], w1_scales[e], "e2m1") for e in range(E)])
    w2 = np.stack([unpack_weight(w2_words[e], w2_scales[e], "e2m1") for e in range(E)])
    xq = mxq(f64(xT)[:, idx], 0, "e4m3")
    h = gelu(by_expert(w1, xq))
    y = by_expert(w2, mxq(h, 0, "e4m3"))
    out = f64(xr).copy()
    out[:, idx] += f64(gate) * y
    return out

@@ -1,0 +1,252 @@
+from contextlib import ExitStack
+
+import concourse.mybir as mybir
+from concourse.masks import make_identity
+
+K, T, E, C, H, N = 1536, 640, 2, 256, 1024, 384
+P = 128
+FLOPS = 2 * E * C * (K * H + H * N)
+
+F32 = mybir.dt.float32
+BF16 = mybir.dt.bfloat16
+I32 = mybir.dt.int32
+U32 = mybir.dt.uint32
+U16 = mybir.dt.uint16
+U8 = mybir.dt.uint8
+FP8X4 = mybir.dt.float8_e4m3fn_x4
+FP4X4 = mybir.dt.float4_e2m1fn_x4
+ACT = mybir.ActivationFunctionType
+MULT = mybir.AluOpType.mult
+
+KP = K // 512
+HP = H // 512
+NB = N // P
+S = E * C // P
+
+
+def tile_moe_res_mlp_gelu_kernel(
+    tc, xT, xr, w1_words, w1_scales, w2_words, w2_scales, gate, offs, out
+):
+    nc = tc.nc
+    with ExitStack() as ctx:
+        keep = ctx.enter_context(tc.tile_pool(name="keep", bufs=1))
+        mmp = ctx.enter_context(tc.psum_pool(name="mmp", bufs=4))
+        xtp = ctx.enter_context(tc.psum_pool(name="xtp", bufs=2))
+        yp = ctx.enter_context(tc.psum_pool(name="yp", bufs=2))
+
+        offsets = keep.tile([P, E * C // 16], U16, name="offsets")
+
+        x_raw = [keep.tile([P, 4, T], F32, align_bytes=64, name="x_raw%d" % s, tag="x_raw%d" % s) for s in range(KP)]
+        x_bf = [keep.tile([P, T, 4], BF16, align_bytes=64, name="x_bf%d" % s, tag="x_bf%d" % s) for s in range(KP)]
+        x_words = [keep.tile([P, T], U32, align_bytes=64, name="x_words%d" % s) for s in range(KP)]
+        x_bytes = [keep.tile([P, T], U8, align_bytes=64, name="x_bytes%d" % s) for s in range(KP)]
+        g_words, g_bytes = {}, {}
+        w1_t = [[keep.tile([P, 2 * H], U8, align_bytes=64, name="w1_%d_%d" % (e, s)) for s in range(KP)] for e in range(E)]
+        w1_s = [keep.tile([P, KP * H], U8, align_bytes=64, name="w1s_%d" % e) for e in range(E)]
+        w2_t = [keep.tile([P, HP * 2 * N], U8, align_bytes=64, name="w2_%d" % e) for e in range(E)]
+        w2_s = keep.tile([P, E * HP * N], U8, align_bytes=64, name="w2s")
+        gate_t = keep.tile([P, NB, E * C], F32, name="gate_t")
+        xr_t = [keep.tile([P, T], F32, name="xr_%d" % m) for m in range(NB)]
+        win = [keep.tile([P, T], F32, name="win_%d" % m) for m in range(NB)]
+        res = [keep.tile([P, T], F32, name="res_%d" % m) for m in range(NB)]
+        h_bf = [keep.tile([P, H], BF16, align_bytes=64, name="h_bf%d" % s) for s in range(S)]
+        h_gr = [keep.tile([P, HP, P, 4], BF16, align_bytes=64, name="h_gr%d" % s) for s in range(S)]
+        h_words = [keep.tile([P, HP * P], U32, align_bytes=64, name="h_words%d" % s) for s in range(S)]
+        h_bytes = [keep.tile([P, HP * P], U8, align_bytes=64, name="h_bytes%d" % s) for s in range(S)]
+        y_g = [keep.tile([P, NB, P], F32, name="y_g%d" % s) for s in range(S)]
+        ident = keep.tile([P, P], F32, name="ident")
+        warm = keep.tile([P, 1], F32, name="warm")
+
+        nc.vector.memset(warm[:], 0.0)
+        nc.scalar.activation(warm[:], warm[:], ACT.Gelu_apprx_tanh)
+        for e in range(E):
+            nc.vector.memset(w1_s[e][:].bitcast(I32), 0)
+        nc.vector.memset(w2_s[:].bitcast(I32), 0)
+        for s in range(KP):
+            nc.gpsimd.memset(x_bytes[s][:].bitcast(I32), 0)
+        make_identity(nc, ident[:])
+        for m in range(NB):
+            nc.gpsimd.memset(win[m][:], 0.0)
+
+        def load_x(s, c0, c1):
+            nc.sync.dma_start(
+                x_raw[s][:, :, c0:c1],
+                xT[512 * s : 512 * (s + 1), :].rearrange("(p j) w -> p j w", j=4)[:, :, c0:c1],
+            )
+
+        def load_w1(e, s):
+            nc.sync.dma_start(w1_t[e][s][:].bitcast(I32), w1_words[e, s].bitcast(I32))
+
+        def load_scales1(e):
+            planes = w1_s[e][:].bitcast(I32).rearrange("p (s c) -> p s c", s=KP)
+            rows = w1_scales[e].bitcast(I32).rearrange("s (q r) c -> r q s c", r=4)
+            for r in range(4):
+                nc.sync.dma_start(planes[r:P:32], rows[r])
+
+        CHUNKS = ((0, 256), (256, 512), (512, T))
+        load_x(0, 0, 256)
+        load_x(0, 256, T)
+        nc.sync.dma_start(offsets[:], offs)
+        load_x(1, 0, T)
+        load_scales1(0)
+        load_w1(0, 0)
+        for c in CHUNKS:
+            load_x(2, *c)
+        load_w1(0, 1)
+        load_w1(0, 2)
+        planes2 = w2_s[:].bitcast(I32).rearrange("p (g c) -> p g c", g=E * HP)
+        rows2 = w2_scales.bitcast(I32).rearrange("e g (q r) c -> r q (e g) c", r=4)
+        for r in range(4):
+            nc.sync.dma_start(planes2[r:P:32], rows2[r])
+        load_scales1(1)
+        for e in range(E):
+            nc.sync.dma_start(
+                w2_t[e][:].bitcast(I32).rearrange("p (g c) -> p g c", g=HP),
+                w2_words[e].bitcast(I32).rearrange("g p c -> p g c"),
+            )
+        for s in range(KP):
+            load_w1(1, s)
+        nc.sync.dma_start(gate_t[:], gate.rearrange("(m p) c -> p m c", p=P))
+        for m in range(NB):
+            nc.sync.dma_start(xr_t[m][:], xr[m * P : (m + 1) * P, :])
+
+        def cast(eng, s, c0, c1):
+            dst = x_bf[s][:, c0:c1, :].rearrange("p (c i) t -> p c t i", i=4)
+            source = x_raw[s][:, :, c0:c1].rearrange("p t (c i) -> p c t i", i=4)
+            if eng == "v":
+                nc.vector.tensor_copy(dst, source)
+            else:
+                nc.scalar.activation(dst, source, ACT.Copy)
+
+        def quant_x(s, c0, c1):
+            nc.vector.quantize_mx(
+                out=x_words[s][:, c0:c1].bitcast(FP8X4),
+                scales=x_bytes[s][:, c0:c1],
+                in_=x_bf[s][:, c0:c1, :].rearrange("p c t -> p (c t)"),
+            )
+
+        def tokens(s):
+            cast("s", s, 0, 256)
+            cast("s", s, 256, 384)
+            cast("v", s, 384, 512)
+            cast("s", s, 512, T)
+            for c in CHUNKS:
+                quant_x(s, *c)
+
+        def gather_tiles(s, e, words_tag, bytes_tag):
+            g_words[s, e] = keep.tile([P, C], U32, align_bytes=64, name="g_words%d_%d" % (s, e), tag=words_tag)
+            g_bytes[s, e] = keep.tile([P, C], U8, align_bytes=64, name="g_bytes%d_%d" % (s, e), tag=bytes_tag)
+
+        def gather(s, e, c0, c1):
+            idx = offsets[:, (e * C + c0) // 16 : (e * C + c1) // 16]
+            nc.vector.tensor_copy(g_words[s, e][:, c0:c1], x_words[s][:].indirect(idx))
+            nc.vector.tensor_copy(g_bytes[s, e][:, c0:c1], x_bytes[s][:].indirect(idx))
+
+        banks = {}
+
+        def mm1(t, s):
+            e, c0 = t // 2, (t % 2) * P
+            for b in range(HP):
+                if s == 0:
+                    banks[t, b] = mmp.tile([P, 512], F32, name="acc")
+                nc.tensor.matmul_mx(
+                    out=banks[t, b][:],
+                    lhsT=g_words[s, e][:, c0 : c0 + P].bitcast(FP8X4),
+                    lhsT_scale=g_bytes[s, e][:, c0 : c0 + P],
+                    rhs=w1_t[e][s][:, b * 1024 : (b + 1) * 1024].bitcast(FP4X4),
+                    rhs_scale=w1_s[e][:, s * H + b * 512 : s * H + (b + 1) * 512],
+                    start=(s == 0),
+                    stop=(s == KP - 1),
+                )
+
+        def hidden(t, engs="ss"):
+            for b in range(HP):
+                nc.scalar.activation(
+                    h_bf[t][:, b * 512 : (b + 1) * 512].rearrange("c (u p e) -> c u p e", u=2, e=2),
+                    banks[t, b][:].rearrange("c (p u e) -> c u p e", u=2, e=2),
+                    ACT.Gelu_apprx_tanh,
+                )
+                xt = xtp.tile([P, 2, P], F32, name="xt")
+                pairs = h_bf[t][:].bitcast(F32)
+                for u in range(2):
+                    nc.tensor.transpose(xt[:, u, :], pairs[:, b * 256 + u * P : b * 256 + (u + 1) * P], ident[:])
+                dst = h_gr[t][:, b].rearrange("p c t -> p (c t)").bitcast(F32).rearrange("p (c u) -> p c u", u=2)
+                source = xt[:].rearrange("p u c -> p c u")
+                if engs[b] == "s":
+                    nc.scalar.copy(dst, source)
+                else:
+                    nc.vector.tensor_copy(dst, source)
+            nc.vector.quantize_mx(
+                out=h_words[t][:].bitcast(FP8X4),
+                scales=h_bytes[t][:],
+                in_=h_gr[t][:].rearrange("p b c t -> p (b c t)"),
+            )
+
+        def mm2(t):
+            e = t // 2
+            y = yp.tile([P, NB, P], F32, name="y")
+            for m in range(NB):
+                for b in range(HP):
+                    w0 = b * N + m * P
+                    nc.tensor.matmul_mx(
+                        out=y[:, m, :],
+                        lhsT=w2_t[e][:, 2 * w0 : 2 * (w0 + P)].bitcast(FP4X4),
+                        lhsT_scale=w2_s[:, e * HP * N + w0 : e * HP * N + w0 + P],
+                        rhs=h_words[t][:, b * P : (b + 1) * P].bitcast(FP8X4),
+                        rhs_scale=h_bytes[t][:, b * P : (b + 1) * P],
+                        start=(b == 0),
+                        stop=(b == HP - 1),
+                    )
+            nc.scalar.copy(y_g[t][:], y[:])
+
+        def scatter(t, m):
+            idx = offsets[:, t * (P // 16) : (t + 1) * (P // 16)]
+            nc.vector.tensor_tensor(win[m][:].indirect(idx), y_g[t][:, m, :], gate_t[:, m, t * P : (t + 1) * P], MULT)
+
+        def finish(m):
+            nc.vector.tensor_tensor(res[m][:], win[m][:], xr_t[m][:], mybir.AluOpType.add)
+            nc.sync.dma_start(out[m * P : (m + 1) * P, :], res[m][:])
+
+        for s in range(KP):
+            gather_tiles(s, 0, "g_words%d_0" % s, "g_bytes%d_0" % s)
+        gather_tiles(0, 1, "g_words0_1", "g_bytes0_1")
+        gather_tiles(2, 1, "g_words2_1", "g_bytes2_1")
+        tokens(0)
+        gather(0, 0, 0, C)
+        gather(0, 1, 0, C)
+        tokens(1)
+        gather(1, 0, 0, C)
+        for t in range(2):
+            mm1(t, 0)
+            mm1(t, 1)
+        tokens(2)
+        for t in range(2):
+            gather(2, 0, t * P, (t + 1) * P)
+            mm1(t, 2)
+        hidden(0, "sv")
+        mm2(0)
+        gather_tiles(1, 1, "x_bf2", "x_raw2")
+        gather(1, 1, 0, C)
+        gather(2, 1, 0, C)
+        hidden(1)
+        mm2(1)
+        for s in range(KP):
+            mm1(2, s)
+        for m in range(NB):
+            scatter(0, m)
+        hidden(2)
+        mm2(2)
+        for s in range(KP):
+            mm1(3, s)
+        for m in range(NB):
+            scatter(1, m)
+        hidden(3)
+        mm2(3)
+        for m in range(NB):
+            scatter(2, m)
+        scatter(3, 0)
+        scatter(3, 1)
+        finish(0)
+        scatter(3, 2)
+        finish(1)
+        finish(2)

@@ -22,6 +22,15 @@ KP = K // 512
 HP = H // 512
 NB = N // P
 S = E * C // P
+BANK = 2048
+HG = 6 * 4 * N
+Y_SLOT = (5, 2, 3, 4)
+CASTS = (
+    (("v", 0, 256), ("v", 256, 384), ("s", 384, 512), ("v", 512, 576), ("s", 576, T)),
+    (("s", 0, 256), ("v", 256, 512), ("v", 512, 576), ("s", 576, T)),
+    (("s", 0, 256), ("s", 256, 384), ("v", 384, 512), ("v", 512, 576), ("s", 576, T)),
+)
+Y_BANK = (1, 0, 2, 1)
 
 
 def tile_moe_res_mlp_gelu_kernel(
@@ -31,29 +40,38 @@ def tile_moe_res_mlp_gelu_kernel(
     with ExitStack() as ctx:
         keep = ctx.enter_context(tc.tile_pool(name="keep", bufs=1))
         mmp = ctx.enter_context(tc.psum_pool(name="mmp", bufs=4))
-        xtp = ctx.enter_context(tc.psum_pool(name="xtp", bufs=2))
-        yp = ctx.enter_context(tc.psum_pool(name="yp", bufs=2))
+        turn = ctx.enter_context(tc.psum_pool(name="turn", bufs=1))
+        relay = ctx.enter_context(tc.tile_pool(name="relay", bufs=1))
 
         offsets = keep.tile([P, E * C // 16], U16, name="offsets")
 
         x_raw = [keep.tile([P, 4, T], F32, align_bytes=64, name="x_raw%d" % s, tag="x_raw%d" % s) for s in range(KP)]
         x_bf = [keep.tile([P, T, 4], BF16, align_bytes=64, name="x_bf%d" % s, tag="x_bf%d" % s) for s in range(KP)]
         x_words = [keep.tile([P, T], U32, align_bytes=64, name="x_words%d" % s) for s in range(KP)]
-        x_bytes = [keep.tile([P, T], U8, align_bytes=64, name="x_bytes%d" % s) for s in range(KP)]
         g_words, g_bytes = {}, {}
-        w1_t = [[keep.tile([P, 2 * H], U8, align_bytes=64, name="w1_%d_%d" % (e, s)) for s in range(KP)] for e in range(E)]
+        xb01 = keep.tile([P, T], U8, align_bytes=64, name="x_bytes01")
+        xb2 = keep.tile([P, T], U8, align_bytes=64, name="x_bytes2")
+        x_planes = (xb01[:], xb01[4:P], xb2[:])
+        for e in range(E):
+            for s in range(2):
+                g_bytes[s, e] = keep.tile([P, C], U8, align_bytes=64, name="g_bytes%d_%d" % (s, e))
+        W1_LOADS = ((0, 0, 1), (0, 1, KP), (1, 0, KP))
+        w1_tiles = [keep.tile([P, (s1 - s0) * 2 * H], U8, align_bytes=64, name="w1_%d_%d" % (e, s0)) for e, s0, s1 in W1_LOADS]
+        w1_t = {}
+        for tl, (e, s0, s1) in zip(w1_tiles, W1_LOADS):
+            for s in range(s0, s1):
+                w1_t[e, s] = (tl, (s - s0) * 2 * H)
         w1_s = [keep.tile([P, KP * H], U8, align_bytes=64, name="w1s_%d" % e) for e in range(E)]
-        w2_t = [keep.tile([P, HP * 2 * N], U8, align_bytes=64, name="w2_%d" % e) for e in range(E)]
+        w2_t = keep.tile([P, E * HP * 2 * N], U8, align_bytes=64, name="w2")
         w2_s = keep.tile([P, E * HP * N], U8, align_bytes=64, name="w2s")
-        gate_t = keep.tile([P, NB, E * C], F32, name="gate_t")
-        xr_t = [keep.tile([P, T], F32, name="xr_%d" % m) for m in range(NB)]
+        gate_t = keep.tile([P, E * C], F32, name="gate_t")
+        xr_t = keep.tile([P, NB, T], F32, name="xr_t")
         win = [keep.tile([P, T], F32, name="win_%d" % m) for m in range(NB)]
         res = [keep.tile([P, T], F32, name="res_%d" % m) for m in range(NB)]
-        h_bf = [keep.tile([P, H], BF16, align_bytes=64, name="h_bf%d" % s) for s in range(S)]
-        h_gr = [keep.tile([P, HP, P, 4], BF16, align_bytes=64, name="h_gr%d" % s) for s in range(S)]
+        h_bf, y_g = {}, {}
+        h_gr = [relay.tile([P, HP, P, 4], BF16, align_bytes=64, name="h_gr%d" % s, offset=HG + s * 2 * H) for s in range(S)]
         h_words = [keep.tile([P, HP * P], U32, align_bytes=64, name="h_words%d" % s) for s in range(S)]
         h_bytes = [keep.tile([P, HP * P], U8, align_bytes=64, name="h_bytes%d" % s) for s in range(S)]
-        y_g = [keep.tile([P, NB, P], F32, name="y_g%d" % s) for s in range(S)]
         ident = keep.tile([P, P], F32, name="ident")
         warm = keep.tile([P, 1], F32, name="warm")
 
@@ -62,8 +80,8 @@ def tile_moe_res_mlp_gelu_kernel(
         for e in range(E):
             nc.vector.memset(w1_s[e][:].bitcast(I32), 0)
         nc.vector.memset(w2_s[:].bitcast(I32), 0)
-        for s in range(KP):
-            nc.gpsimd.memset(x_bytes[s][:].bitcast(I32), 0)
+        for plane in (xb01, xb2, g_bytes[1, 0], g_bytes[1, 1]):
+            nc.gpsimd.memset(plane[:].bitcast(I32), 0)
         make_identity(nc, ident[:])
         for m in range(NB):
             nc.gpsimd.memset(win[m][:], 0.0)
@@ -74,8 +92,12 @@ def tile_moe_res_mlp_gelu_kernel(
                 xT[512 * s : 512 * (s + 1), :].rearrange("(p j) w -> p j w", j=4)[:, :, c0:c1],
             )
 
-        def load_w1(e, s):
-            nc.sync.dma_start(w1_t[e][s][:].bitcast(I32), w1_words[e, s].bitcast(I32))
+        def load_w1(i):
+            e, s0, s1 = W1_LOADS[i]
+            nc.sync.dma_start(
+                w1_tiles[i][:].bitcast(I32).rearrange("p (s c) -> p s c", s=s1 - s0),
+                w1_words[e, s0:s1].bitcast(I32).rearrange("s p c -> p s c"),
+            )
 
         def load_scales1(e):
             planes = w1_s[e][:].bitcast(I32).rearrange("p (s c) -> p s c", s=KP)
@@ -84,31 +106,30 @@ def tile_moe_res_mlp_gelu_kernel(
                 nc.sync.dma_start(planes[r:P:32], rows[r])
 
         CHUNKS = ((0, 256), (256, 512), (512, T))
-        load_x(0, 0, 256)
-        load_x(0, 256, T)
+        for c in CHUNKS:
+            load_x(0, *c)
         nc.sync.dma_start(offsets[:], offs)
-        load_x(1, 0, T)
+        for c in CHUNKS:
+            load_x(1, *c)
         load_scales1(0)
-        load_w1(0, 0)
+        load_w1(0)
         for c in CHUNKS:
             load_x(2, *c)
-        load_w1(0, 1)
-        load_w1(0, 2)
-        planes2 = w2_s[:].bitcast(I32).rearrange("p (g c) -> p g c", g=E * HP)
-        rows2 = w2_scales.bitcast(I32).rearrange("e g (q r) c -> r q (e g) c", r=4)
-        for r in range(4):
-            nc.sync.dma_start(planes2[r:P:32], rows2[r])
-        load_scales1(1)
-        for e in range(E):
+        load_w1(1)
+
+        def late_loads():
+            planes2 = w2_s[:].bitcast(I32).rearrange("p (g c) -> p g c", g=E * HP)
+            rows2 = w2_scales.bitcast(I32).rearrange("e g (q r) c -> r q (e g) c", r=4)
             nc.sync.dma_start(
-                w2_t[e][:].bitcast(I32).rearrange("p (g c) -> p g c", g=HP),
-                w2_words[e].bitcast(I32).rearrange("g p c -> p g c"),
+                w2_t[:].bitcast(I32).rearrange("p (g c) -> p g c", g=E * HP),
+                w2_words.bitcast(I32).rearrange("e g p c -> p (e g) c"),
             )
-        for s in range(KP):
-            load_w1(1, s)
-        nc.sync.dma_start(gate_t[:], gate.rearrange("(m p) c -> p m c", p=P))
-        for m in range(NB):
-            nc.sync.dma_start(xr_t[m][:], xr[m * P : (m + 1) * P, :])
+            for r in range(4):
+                nc.sync.dma_start(planes2[r:P:32], rows2[r])
+            nc.sync.dma_start(gate_t[:], gate[0:P, :])
+            load_w1(2)
+            load_scales1(1)
+            nc.sync.dma_start(xr_t[:], xr.rearrange("(m p) c -> p m c", p=P))
 
         def cast(eng, s, c0, c1):
             dst = x_bf[s][:, c0:c1, :].rearrange("p (c i) t -> p c t i", i=4)
@@ -121,127 +142,171 @@ def tile_moe_res_mlp_gelu_kernel(
         def quant_x(s, c0, c1):
             nc.vector.quantize_mx(
                 out=x_words[s][:, c0:c1].bitcast(FP8X4),
-                scales=x_bytes[s][:, c0:c1],
+                scales=x_planes[s][:, c0:c1],
                 in_=x_bf[s][:, c0:c1, :].rearrange("p c t -> p (c t)"),
             )
 
         def tokens(s):
-            cast("s", s, 0, 256)
-            cast("s", s, 256, 384)
-            cast("v", s, 384, 512)
-            cast("s", s, 512, T)
+            for eng, c0, c1 in CASTS[s]:
+                cast(eng, s, c0, c1)
             for c in CHUNKS:
                 quant_x(s, *c)
 
-        def gather_tiles(s, e, words_tag, bytes_tag):
-            g_words[s, e] = keep.tile([P, C], U32, align_bytes=64, name="g_words%d_%d" % (s, e), tag=words_tag)
-            g_bytes[s, e] = keep.tile([P, C], U8, align_bytes=64, name="g_bytes%d_%d" % (s, e), tag=bytes_tag)
+        def slots(e, c0, c1):
+            return offsets[:, (e * C + c0) // 16 : (e * C + c1) // 16]
 
-        def gather(s, e, c0, c1):
-            idx = offsets[:, (e * C + c0) // 16 : (e * C + c1) // 16]
-            nc.vector.tensor_copy(g_words[s, e][:, c0:c1], x_words[s][:].indirect(idx))
-            nc.vector.tensor_copy(g_bytes[s, e][:, c0:c1], x_bytes[s][:].indirect(idx))
+        def gather_words(s, e, c0, c1):
+            nc.vector.tensor_copy(g_words[s, e][:, c0:c1], x_words[s][:].indirect(slots(e, c0, c1)))
+
+        last = {}
+
+        def gather_last(t, pool, place_words=None, place_bytes=None):
+            words = pool.tile([P, P], U32, align_bytes=64, name="last_words%d" % t, offset=place_words)
+            plane = pool.tile([P, P], U8, align_bytes=64, name="last_bytes%d" % t, offset=place_bytes)
+            idx = offsets[:, t * P // 16 : (t + 1) * P // 16]
+            nc.vector.tensor_copy(words[:], x_words[KP - 1][:].indirect(idx))
+            nc.vector.tensor_copy(plane[:], xb2[:].indirect(idx))
+            last[t] = (words[:], plane[:])
+
+        def operand(s, t):
+            if s == KP - 1:
+                return last[t]
+            e, c0 = t // 2, (t % 2) * P
+            return g_words[s, e][:, c0 : c0 + P], g_bytes[s, e][:, c0 : c0 + P]
+
+        def gather_pair(e):
+            nc.vector.tensor_copy(g_bytes[0, e][:], xb01[:].indirect(slots(e, 0, C)))
+
+        def lower_rows(e, queue):
+            queue.dma_start(g_bytes[1, e][0 : P - 4].bitcast(I32), g_bytes[0, e][4:P].bitcast(I32))
 
         banks = {}
 
-        def mm1(t, s):
-            e, c0 = t // 2, (t % 2) * P
-            for b in range(HP):
+        def mm1(t, s, halves=range(HP)):
+            e = t // 2
+            words, plane = operand(s, t)
+            for b in halves:
                 if s == 0:
                     banks[t, b] = mmp.tile([P, 512], F32, name="acc")
                 nc.tensor.matmul_mx(
                     out=banks[t, b][:],
-                    lhsT=g_words[s, e][:, c0 : c0 + P].bitcast(FP8X4),
-                    lhsT_scale=g_bytes[s, e][:, c0 : c0 + P],
-                    rhs=w1_t[e][s][:, b * 1024 : (b + 1) * 1024].bitcast(FP4X4),
+                    lhsT=words.bitcast(FP8X4),
+                    lhsT_scale=plane,
+                    rhs=w1_t[e, s][0][:, w1_t[e, s][1] + b * 1024 : w1_t[e, s][1] + (b + 1) * 1024].bitcast(FP4X4),
                     rhs_scale=w1_s[e][:, s * H + b * 512 : s * H + (b + 1) * 512],
                     start=(s == 0),
                     stop=(s == KP - 1),
                 )
 
+        def quant_h(t, b0, b1):
+            nc.vector.quantize_mx(
+                out=h_words[t][:, b0 * P : b1 * P].bitcast(FP8X4),
+                scales=h_bytes[t][:, b0 * P : b1 * P],
+                in_=h_gr[t][:, b0:b1].rearrange("p b c t -> p (b c t)"),
+            )
+
         def hidden(t, engs="ss"):
             for b in range(HP):
+                if b == HP - 1:
+                    h_bf[t, b] = relay.tile([P, 512], BF16, align_bytes=64, name="h_bf%d_%d" % (t, b), offset=t * 4 * N)
+                else:
+                    h_bf[t, b] = keep.tile([P, 512], BF16, align_bytes=64, name="h_bf%d_%d" % (t, b))
                 nc.scalar.activation(
-                    h_bf[t][:, b * 512 : (b + 1) * 512].rearrange("c (u p e) -> c u p e", u=2, e=2),
+                    h_bf[t, b][:].rearrange("c (u p e) -> c u p e", u=2, e=2),
                     banks[t, b][:].rearrange("c (p u e) -> c u p e", u=2, e=2),
                     ACT.Gelu_apprx_tanh,
                 )
-                xt = xtp.tile([P, 2, P], F32, name="xt")
-                pairs = h_bf[t][:].bitcast(F32)
+                xt = turn.tile([P, 2, P], F32, name="xt%d_%d" % (t, b), offset=BANK * (2 * (t % 2) + b))
+                pairs = h_bf[t, b][:].bitcast(F32)
                 for u in range(2):
-                    nc.tensor.transpose(xt[:, u, :], pairs[:, b * 256 + u * P : b * 256 + (u + 1) * P], ident[:])
+                    nc.tensor.transpose(xt[:, u, :], pairs[:, u * P : (u + 1) * P], ident[:])
                 dst = h_gr[t][:, b].rearrange("p c t -> p (c t)").bitcast(F32).rearrange("p (c u) -> p c u", u=2)
                 source = xt[:].rearrange("p u c -> p c u")
                 if engs[b] == "s":
                     nc.scalar.copy(dst, source)
                 else:
                     nc.vector.tensor_copy(dst, source)
-            nc.vector.quantize_mx(
-                out=h_words[t][:].bitcast(FP8X4),
-                scales=h_bytes[t][:],
-                in_=h_gr[t][:].rearrange("p b c t -> p (b c t)"),
-            )
+                if t == 0:
+                    quant_h(t, b, b + 1)
+            if t > 0:
+                quant_h(t, 0, HP)
 
-        def mm2(t):
+        def mm2(t, m, y):
             e = t // 2
-            y = yp.tile([P, NB, P], F32, name="y")
-            for m in range(NB):
-                for b in range(HP):
-                    w0 = b * N + m * P
-                    nc.tensor.matmul_mx(
-                        out=y[:, m, :],
-                        lhsT=w2_t[e][:, 2 * w0 : 2 * (w0 + P)].bitcast(FP4X4),
-                        lhsT_scale=w2_s[:, e * HP * N + w0 : e * HP * N + w0 + P],
-                        rhs=h_words[t][:, b * P : (b + 1) * P].bitcast(FP8X4),
-                        rhs_scale=h_bytes[t][:, b * P : (b + 1) * P],
-                        start=(b == 0),
-                        stop=(b == HP - 1),
-                    )
-            nc.scalar.copy(y_g[t][:], y[:])
+            for b in range(HP):
+                w0 = (e * HP + b) * N + m * P
+                nc.tensor.matmul_mx(
+                    out=y,
+                    lhsT=w2_t[:, 2 * w0 : 2 * (w0 + P)].bitcast(FP4X4),
+                    lhsT_scale=w2_s[:, w0 : w0 + P],
+                    rhs=h_words[t][:, b * P : (b + 1) * P].bitcast(FP8X4),
+                    rhs_scale=h_bytes[t][:, b * P : (b + 1) * P],
+                    start=(b == 0),
+                    stop=(b == HP - 1),
+                )
+
+        def layer2(t, m0, m1, bank):
+            y = turn.tile([P, m1 - m0, P], F32, name="y%d_%d" % (t, m0), offset=BANK * bank)
+            for m in range(m0, m1):
+                mm2(t, m, y[:, m - m0, :])
+            nc.scalar.copy(y_g[t][:, m0:m1, :], y[:])
+
+        def y_tile(t):
+            y_g[t] = relay.tile([P, NB, P], F32, align_bytes=64, name="y_g%d" % t, offset=Y_SLOT[t] * 4 * N)
 
         def scatter(t, m):
             idx = offsets[:, t * (P // 16) : (t + 1) * (P // 16)]
-            nc.vector.tensor_tensor(win[m][:].indirect(idx), y_g[t][:, m, :], gate_t[:, m, t * P : (t + 1) * P], MULT)
+            nc.vector.tensor_tensor(win[m][:].indirect(idx), y_g[t][:, m, :], gate_t[:, t * P : (t + 1) * P], MULT)
 
         def finish(m):
-            nc.vector.tensor_tensor(res[m][:], win[m][:], xr_t[m][:], mybir.AluOpType.add)
+            nc.vector.tensor_tensor(res[m][:], win[m][:], xr_t[:, m, :], mybir.AluOpType.add)
             nc.sync.dma_start(out[m * P : (m + 1) * P, :], res[m][:])
 
-        for s in range(KP):
-            gather_tiles(s, 0, "g_words%d_0" % s, "g_bytes%d_0" % s)
-        gather_tiles(0, 1, "g_words0_1", "g_bytes0_1")
-        gather_tiles(2, 1, "g_words2_1", "g_bytes2_1")
+        for s, e in ((0, 0), (0, 1), (1, 0)):
+            g_words[s, e] = keep.tile([P, C], U32, align_bytes=64, name="g_words%d_%d" % (s, e))
         tokens(0)
-        gather(0, 0, 0, C)
-        gather(0, 1, 0, C)
+        gather_words(0, 0, 0, C)
+        gather_words(0, 1, 0, C)
         tokens(1)
-        gather(1, 0, 0, C)
+        gather_pair(0)
+        lower_rows(0, nc.sync)
+        gather_words(1, 0, 0, C)
+        gather_pair(1)
+        lower_rows(1, nc.gpsimd)
+        late_loads()
         for t in range(2):
             mm1(t, 0)
-            mm1(t, 1)
         tokens(2)
         for t in range(2):
-            gather(2, 0, t * P, (t + 1) * P)
-            mm1(t, 2)
-        hidden(0, "sv")
-        mm2(0)
-        gather_tiles(1, 1, "x_bf2", "x_raw2")
-        gather(1, 1, 0, C)
-        gather(2, 1, 0, C)
+            gather_last(t, keep)
+            for b in range(HP):
+                mm1(t, 1, (b,))
+                mm1(t, 2, (b,))
+        hidden(0, "vv")
+        y_tile(0)
+        layer2(0, 0, 1, 0)
+        layer2(0, 1, NB, 1)
+        g_words[1, 1] = keep.tile([P, C], U32, align_bytes=64, name="g_words1_1", tag="x_bf2")
+        gather_words(1, 1, 0, C)
+        gather_last(2, keep)
+        gather_last(3, relay, HG + H, HG + H + 4 * P)
         hidden(1)
-        mm2(1)
         for s in range(KP):
             mm1(2, s)
         for m in range(NB):
             scatter(0, m)
         hidden(2)
-        mm2(2)
+        y_tile(1)
+        layer2(1, 0, NB, Y_BANK[1])
         for s in range(KP):
             mm1(3, s)
         for m in range(NB):
             scatter(1, m)
         hidden(3)
-        mm2(3)
+        y_tile(2)
+        layer2(2, 0, NB, Y_BANK[2])
+        y_tile(3)
+        layer2(3, 0, NB, Y_BANK[3])
         for m in range(NB):
             scatter(2, m)
         scatter(3, 0)

@@ -23,14 +23,14 @@ HP = H // 512
 NB = N // P
 S = E * C // P
 BANK = 2048
+LATE = 2
+TB = T // P
 HG = 6 * 4 * N
-Y_SLOT = (5, 2, 3, 4)
 CASTS = (
-    (("v", 0, 256), ("v", 256, 384), ("s", 384, 512), ("v", 512, 576), ("s", 576, T)),
-    (("s", 0, 256), ("v", 256, 512), ("v", 512, 576), ("s", 576, T)),
+    (("v", 0, 256), ("v", 256, 512), ("s", 512, T)),
+    (("s", 0, 256), ("v", 256, 512), ("s", 512, T)),
     (("s", 0, 256), ("s", 256, 384), ("v", 384, 512), ("v", 512, 576), ("s", 576, T)),
 )
-Y_BANK = (1, 0, 2, 1)
 
 
 def tile_moe_res_mlp_gelu_kernel(
@@ -39,7 +39,6 @@ def tile_moe_res_mlp_gelu_kernel(
     nc = tc.nc
     with ExitStack() as ctx:
         keep = ctx.enter_context(tc.tile_pool(name="keep", bufs=1))
-        mmp = ctx.enter_context(tc.psum_pool(name="mmp", bufs=4))
         turn = ctx.enter_context(tc.psum_pool(name="turn", bufs=1))
         relay = ctx.enter_context(tc.tile_pool(name="relay", bufs=1))
 
@@ -49,26 +48,26 @@ def tile_moe_res_mlp_gelu_kernel(
         x_bf = [keep.tile([P, T, 4], BF16, align_bytes=64, name="x_bf%d" % s, tag="x_bf%d" % s) for s in range(KP)]
         x_words = [keep.tile([P, T], U32, align_bytes=64, name="x_words%d" % s) for s in range(KP)]
         g_words, g_bytes = {}, {}
-        xb01 = keep.tile([P, T], U8, align_bytes=64, name="x_bytes01")
-        xb2 = keep.tile([P, T], U8, align_bytes=64, name="x_bytes2")
-        x_planes = (xb01[:], xb01[4:P], xb2[:])
-        for e in range(E):
-            for s in range(2):
-                g_bytes[s, e] = keep.tile([P, C], U8, align_bytes=64, name="g_bytes%d_%d" % (s, e))
-        W1_LOADS = ((0, 0, 1), (0, 1, KP), (1, 0, KP))
+        x_bytes = [keep.tile([P, T], U8, align_bytes=64, name="x_bytes%d" % s) for s in range(KP)]
+        W1_LOADS = ((0, 0, 1), (0, 1, 2), (0, 2, 3), (1, 0, KP))
         w1_tiles = [keep.tile([P, (s1 - s0) * 2 * H], U8, align_bytes=64, name="w1_%d_%d" % (e, s0)) for e, s0, s1 in W1_LOADS]
         w1_t = {}
         for tl, (e, s0, s1) in zip(w1_tiles, W1_LOADS):
             for s in range(s0, s1):
                 w1_t[e, s] = (tl, (s - s0) * 2 * H)
-        w1_s = [keep.tile([P, KP * H], U8, align_bytes=64, name="w1s_%d" % e) for e in range(E)]
+        S1_LOADS = ((0, 0, 1), (0, 1, KP), (1, 0, KP))
+        s1_tiles = [keep.tile([P, (s1 - s0) * H], U8, align_bytes=64, name="w1s_%d_%d" % (e, s0)) for e, s0, s1 in S1_LOADS]
+        w1_s = {}
+        for tl, (e, s0, s1) in zip(s1_tiles, S1_LOADS):
+            for s in range(s0, s1):
+                w1_s[e, s] = tl[:, (s - s0) * H : (s - s0 + 1) * H]
         w2_t = keep.tile([P, E * HP * 2 * N], U8, align_bytes=64, name="w2")
         w2_s = keep.tile([P, E * HP * N], U8, align_bytes=64, name="w2s")
         gate_t = keep.tile([P, E * C], F32, name="gate_t")
         xr_t = keep.tile([P, NB, T], F32, name="xr_t")
         win = [keep.tile([P, T], F32, name="win_%d" % m) for m in range(NB)]
         res = [keep.tile([P, T], F32, name="res_%d" % m) for m in range(NB)]
-        h_bf, y_g = {}, {}
+        h_bf, y_ps, y_g = {}, {}, {}
         h_gr = [relay.tile([P, HP, P, 4], BF16, align_bytes=64, name="h_gr%d" % s, offset=HG + s * 2 * H) for s in range(S)]
         h_words = [keep.tile([P, HP * P], U32, align_bytes=64, name="h_words%d" % s) for s in range(S)]
         h_bytes = [keep.tile([P, HP * P], U8, align_bytes=64, name="h_bytes%d" % s) for s in range(S)]
@@ -77,10 +76,10 @@ def tile_moe_res_mlp_gelu_kernel(
 
         nc.vector.memset(warm[:], 0.0)
         nc.scalar.activation(warm[:], warm[:], ACT.Gelu_apprx_tanh)
-        for e in range(E):
-            nc.vector.memset(w1_s[e][:].bitcast(I32), 0)
+        for tl in s1_tiles:
+            nc.vector.memset(tl[:].bitcast(I32), 0)
         nc.vector.memset(w2_s[:].bitcast(I32), 0)
-        for plane in (xb01, xb2, g_bytes[1, 0], g_bytes[1, 1]):
+        for plane in x_bytes:
             nc.gpsimd.memset(plane[:].bitcast(I32), 0)
         make_identity(nc, ident[:])
         for m in range(NB):
@@ -99,37 +98,37 @@ def tile_moe_res_mlp_gelu_kernel(
                 w1_words[e, s0:s1].bitcast(I32).rearrange("s p c -> p s c"),
             )
 
-        def load_scales1(e):
-            planes = w1_s[e][:].bitcast(I32).rearrange("p (s c) -> p s c", s=KP)
-            rows = w1_scales[e].bitcast(I32).rearrange("s (q r) c -> r q s c", r=4)
+        def load_scales1(i):
+            e, s0, s1 = S1_LOADS[i]
+            planes = s1_tiles[i][:].bitcast(I32).rearrange("p (s c) -> p s c", s=s1 - s0)
+            rows = w1_scales[e, s0:s1].bitcast(I32).rearrange("s (q r) c -> r q s c", r=4)
             for r in range(4):
                 nc.sync.dma_start(planes[r:P:32], rows[r])
 
         CHUNKS = ((0, 256), (256, 512), (512, T))
-        for c in CHUNKS:
-            load_x(0, *c)
+        load_x(0, 0, 256)
+        load_x(0, 256, T)
         nc.sync.dma_start(offsets[:], offs)
-        for c in CHUNKS:
-            load_x(1, *c)
+        load_x(1, 0, T)
         load_scales1(0)
         load_w1(0)
         for c in CHUNKS:
             load_x(2, *c)
+        load_scales1(1)
         load_w1(1)
-
-        def late_loads():
-            planes2 = w2_s[:].bitcast(I32).rearrange("p (g c) -> p g c", g=E * HP)
-            rows2 = w2_scales.bitcast(I32).rearrange("e g (q r) c -> r q (e g) c", r=4)
-            nc.sync.dma_start(
-                w2_t[:].bitcast(I32).rearrange("p (g c) -> p g c", g=E * HP),
-                w2_words.bitcast(I32).rearrange("e g p c -> p (e g) c"),
-            )
-            for r in range(4):
-                nc.sync.dma_start(planes2[r:P:32], rows2[r])
-            nc.sync.dma_start(gate_t[:], gate[0:P, :])
-            load_w1(2)
-            load_scales1(1)
-            nc.sync.dma_start(xr_t[:], xr.rearrange("(m p) c -> p m c", p=P))
+        load_w1(2)
+        planes2 = w2_s[:].bitcast(I32).rearrange("p (g c) -> p g c", g=E * HP)
+        rows2 = w2_scales.bitcast(I32).rearrange("e g (q r) c -> r q (e g) c", r=4)
+        nc.sync.dma_start(
+            w2_t[:].bitcast(I32).rearrange("p (g c) -> p g c", g=E * HP),
+            w2_words.bitcast(I32).rearrange("e g p c -> p (e g) c"),
+        )
+        for r in range(4):
+            nc.sync.dma_start(planes2[r:P:32], rows2[r])
+        load_w1(3)
+        load_scales1(2)
+        nc.sync.dma_start(gate_t[:], gate[0:P, :])
+        nc.sync.dma_start(xr_t[:], xr.rearrange("(m p) c -> p m c", p=P))
 
         def cast(eng, s, c0, c1):
             dst = x_bf[s][:, c0:c1, :].rearrange("p (c i) t -> p c t i", i=4)
@@ -142,7 +141,7 @@ def tile_moe_res_mlp_gelu_kernel(
         def quant_x(s, c0, c1):
             nc.vector.quantize_mx(
                 out=x_words[s][:, c0:c1].bitcast(FP8X4),
-                scales=x_planes[s][:, c0:c1],
+                scales=x_bytes[s][:, c0:c1],
                 in_=x_bf[s][:, c0:c1, :].rearrange("p c t -> p (c t)"),
             )
 
@@ -152,11 +151,12 @@ def tile_moe_res_mlp_gelu_kernel(
             for c in CHUNKS:
                 quant_x(s, *c)
 
-        def slots(e, c0, c1):
-            return offsets[:, (e * C + c0) // 16 : (e * C + c1) // 16]
-
-        def gather_words(s, e, c0, c1):
-            nc.vector.tensor_copy(g_words[s, e][:, c0:c1], x_words[s][:].indirect(slots(e, c0, c1)))
+        def gather(s, e, words_tag=None, bytes_tag=None):
+            g_words[s, e] = keep.tile([P, C], U32, align_bytes=64, name="g_words%d_%d" % (s, e), tag=words_tag)
+            g_bytes[s, e] = keep.tile([P, C], U8, align_bytes=64, name="g_bytes%d_%d" % (s, e), tag=bytes_tag)
+            idx = offsets[:, e * C // 16 : (e + 1) * C // 16]
+            nc.vector.tensor_copy(g_words[s, e][:], x_words[s][:].indirect(idx))
+            nc.vector.tensor_copy(g_bytes[s, e][:], x_bytes[s][:].indirect(idx))
 
         last = {}
 
@@ -165,7 +165,7 @@ def tile_moe_res_mlp_gelu_kernel(
             plane = pool.tile([P, P], U8, align_bytes=64, name="last_bytes%d" % t, offset=place_bytes)
             idx = offsets[:, t * P // 16 : (t + 1) * P // 16]
             nc.vector.tensor_copy(words[:], x_words[KP - 1][:].indirect(idx))
-            nc.vector.tensor_copy(plane[:], xb2[:].indirect(idx))
+            nc.vector.tensor_copy(plane[:], x_bytes[KP - 1][:].indirect(idx))
             last[t] = (words[:], plane[:])
 
         def operand(s, t):
@@ -174,12 +174,6 @@ def tile_moe_res_mlp_gelu_kernel(
             e, c0 = t // 2, (t % 2) * P
             return g_words[s, e][:, c0 : c0 + P], g_bytes[s, e][:, c0 : c0 + P]
 
-        def gather_pair(e):
-            nc.vector.tensor_copy(g_bytes[0, e][:], xb01[:].indirect(slots(e, 0, C)))
-
-        def lower_rows(e, queue):
-            queue.dma_start(g_bytes[1, e][0 : P - 4].bitcast(I32), g_bytes[0, e][4:P].bitcast(I32))
-
         banks = {}
 
         def mm1(t, s, halves=range(HP)):
@@ -187,13 +181,13 @@ def tile_moe_res_mlp_gelu_kernel(
             words, plane = operand(s, t)
             for b in halves:
                 if s == 0:
-                    banks[t, b] = mmp.tile([P, 512], F32, name="acc")
+                    banks[t, b] = turn.tile([P, 512], F32, name="acc%d_%d" % (t, b), offset=BANK * (2 * (t % 2) + b))
                 nc.tensor.matmul_mx(
                     out=banks[t, b][:],
                     lhsT=words.bitcast(FP8X4),
                     lhsT_scale=plane,
                     rhs=w1_t[e, s][0][:, w1_t[e, s][1] + b * 1024 : w1_t[e, s][1] + (b + 1) * 1024].bitcast(FP4X4),
-                    rhs_scale=w1_s[e][:, s * H + b * 512 : s * H + (b + 1) * 512],
+                    rhs_scale=w1_s[e, s][:, b * 512 : (b + 1) * 512],
                     start=(s == 0),
                     stop=(s == KP - 1),
                 )
@@ -216,7 +210,7 @@ def tile_moe_res_mlp_gelu_kernel(
                     banks[t, b][:].rearrange("c (p u e) -> c u p e", u=2, e=2),
                     ACT.Gelu_apprx_tanh,
                 )
-                xt = turn.tile([P, 2, P], F32, name="xt%d_%d" % (t, b), offset=BANK * (2 * (t % 2) + b))
+                xt = turn.tile([P, 2, P], F32, name="xt%d_%d" % (t, b), offset=BANK * (4 + 2 * (t % 2) + b))
                 pairs = h_bf[t, b][:].bitcast(F32)
                 for u in range(2):
                     nc.tensor.transpose(xt[:, u, :], pairs[:, u * P : (u + 1) * P], ident[:])
@@ -249,69 +243,98 @@ def tile_moe_res_mlp_gelu_kernel(
             y = turn.tile([P, m1 - m0, P], F32, name="y%d_%d" % (t, m0), offset=BANK * bank)
             for m in range(m0, m1):
                 mm2(t, m, y[:, m - m0, :])
-            nc.scalar.copy(y_g[t][:, m0:m1, :], y[:])
+                y_ps[t, m] = (y, m - m0)
 
-        def y_tile(t):
-            y_g[t] = relay.tile([P, NB, P], F32, align_bytes=64, name="y_g%d" % t, offset=Y_SLOT[t] * 4 * N)
+        def y_out(t, m0, m1, pool, place=None):
+            y_sb = pool.tile([P, m1 - m0, P], F32, align_bytes=64, name="y_sb%d_%d" % (t, m0), offset=place)
+            y, i = y_ps[t, m0]
+            nc.scalar.copy(y_sb[:], y[:, i : i + m1 - m0, :])
+            for m in range(m0, m1):
+                y_g[t, m] = y_sb[:, m - m0, :]
 
         def scatter(t, m):
             idx = offsets[:, t * (P // 16) : (t + 1) * (P // 16)]
-            nc.vector.tensor_tensor(win[m][:].indirect(idx), y_g[t][:, m, :], gate_t[:, t * P : (t + 1) * P], MULT)
+            nc.vector.tensor_tensor(win[m][:].indirect(idx), y_g[t, m], gate_t[:, t * P : (t + 1) * P], MULT)
 
         def finish(m):
             nc.vector.tensor_tensor(res[m][:], win[m][:], xr_t[:, m, :], mybir.AluOpType.add)
             nc.sync.dma_start(out[m * P : (m + 1) * P, :], res[m][:])
 
-        for s, e in ((0, 0), (0, 1), (1, 0)):
-            g_words[s, e] = keep.tile([P, C], U32, align_bytes=64, name="g_words%d_%d" % (s, e))
+        def last_block():
+            m = NB - 1
+            y = turn.tile([P, S - LATE, P], F32, name="y_last", offset=BANK * 7)
+            for t in range(LATE, S):
+                mm2(t, m, y[:, t - LATE, :])
+            y_sb = keep.tile([P, (S - LATE) * P], F32, name="y_last_sb")
+            nc.scalar.copy(y_sb[:], y[:].rearrange("p t c -> p (t c)"))
+            nc.vector.tensor_tensor(win[m][:].indirect(offsets[:, LATE * P // 16 :]), y_sb[:], gate_t[:, LATE * P :], MULT)
+            finish(m)
+
+        PIECES = ((0, 3), (3, TB))
+
+        def sum_turned(m):
+            turned = keep.tile([P, TB, P], F32, name="turned%d" % m)
+            for i, (j0, j1) in enumerate(PIECES):
+                acc = turn.tile([P, 512], F32, name="sum%d" % i, offset=BANK * i)
+                for j in range(j0, j1):
+                    o = acc[:, (j - j0) * P : (j - j0 + 1) * P]
+                    nc.tensor.matmul(o, xr_t[:, m, j * P : (j + 1) * P], ident[:], start=True, stop=False, is_transpose=True)
+                    nc.tensor.matmul(o, win[m][:, j * P : (j + 1) * P], ident[:], start=False, stop=True, is_transpose=True)
+                nc.scalar.copy(turned[:, j0:j1, :].rearrange("p j c -> p (j c)"), acc[:, 0 : (j1 - j0) * P])
+            return turned
+
+        def turn_back(m, turned):
+            for i, (j0, j1) in enumerate(PIECES):
+                acc = turn.tile([P, 512], F32, name="back%d" % i, offset=BANK * (2 + i))
+                for j in range(j0, j1):
+                    nc.tensor.transpose(acc[:, (j - j0) * P : (j - j0 + 1) * P], turned[:, j, :], ident[:])
+                nc.scalar.copy(res[m][:, j0 * P : j1 * P], acc[:, 0 : (j1 - j0) * P])
+                nc.sync.dma_start(out[m * P : (m + 1) * P, j0 * P : j1 * P], res[m][:, j0 * P : j1 * P])
+
         tokens(0)
-        gather_words(0, 0, 0, C)
-        gather_words(0, 1, 0, C)
+        gather(0, 0, "gw00", "gb00")
+        gather(0, 1, "gw01", "gb01")
         tokens(1)
-        gather_pair(0)
-        lower_rows(0, nc.sync)
-        gather_words(1, 0, 0, C)
-        gather_pair(1)
-        lower_rows(1, nc.gpsimd)
-        late_loads()
+        gather(1, 0, "gw10", "gb10")
         for t in range(2):
             mm1(t, 0)
         tokens(2)
         for t in range(2):
             gather_last(t, keep)
-            for b in range(HP):
-                mm1(t, 1, (b,))
-                mm1(t, 2, (b,))
+            mm1(t, 1)
+            mm1(t, 2)
         hidden(0, "vv")
-        y_tile(0)
-        layer2(0, 0, 1, 0)
-        layer2(0, 1, NB, 1)
-        g_words[1, 1] = keep.tile([P, C], U32, align_bytes=64, name="g_words1_1", tag="x_bf2")
-        gather_words(1, 1, 0, C)
-        gather_last(2, keep)
+        layer2(0, 0, 1, 4)
+        y_out(0, 0, 1, keep)
+        layer2(0, 1, NB, 5)
+        y_out(0, 1, NB, keep)
+        gather(1, 1, "x_bf2", "x_raw2")
+        gather_last(2, relay, HG, HG + 4 * P)
         gather_last(3, relay, HG + H, HG + H + 4 * P)
         hidden(1)
-        for s in range(KP):
-            mm1(2, s)
+        for b in range(HP):
+            for s in range(KP):
+                mm1(2, s, (b,))
         for m in range(NB):
             scatter(0, m)
         hidden(2)
-        y_tile(1)
-        layer2(1, 0, NB, Y_BANK[1])
-        for s in range(KP):
-            mm1(3, s)
+        layer2(1, 0, NB, 0)
+        y_out(1, 0, 2, keep)
+        y_out(1, 2, NB, relay, 2 * 4 * N)
+        for b in range(HP):
+            for s in range(KP):
+                mm1(3, s, (b,))
         for m in range(NB):
             scatter(1, m)
         hidden(3)
-        y_tile(2)
-        layer2(2, 0, NB, Y_BANK[2])
-        y_tile(3)
-        layer2(3, 0, NB, Y_BANK[3])
-        for m in range(NB):
-            scatter(2, m)
+        layer2(2, 0, NB - 1, 6)
+        y_out(2, 0, NB - 1, relay, 3 * 4 * N)
+        layer2(3, 0, NB - 1, 5)
+        y_out(3, 0, NB - 1, keep)
+        scatter(2, 0)
+        scatter(2, 1)
         scatter(3, 0)
         scatter(3, 1)
-        finish(0)
-        scatter(3, 2)
         finish(1)
-        finish(2)
+        last_block()
+        turn_back(0, sum_turned(0))

@@ -28,7 +28,7 @@ TB = T // P
 HG = 6 * 4 * N
 CASTS = (
     (("v", 0, 256), ("v", 256, 512), ("s", 512, T)),
-    (("s", 0, 256), ("v", 256, 512), ("s", 512, T)),
+    (("s", 0, 256), ("s", 256, 512), ("v", 512, T)),
     (("s", 0, 256), ("s", 256, 384), ("v", 384, 512), ("v", 512, 576), ("s", 576, T)),
 )
 
@@ -61,7 +61,7 @@ def tile_moe_res_mlp_gelu_kernel(
         for tl, (e, s0, s1) in zip(s1_tiles, S1_LOADS):
             for s in range(s0, s1):
                 w1_s[e, s] = tl[:, (s - s0) * H : (s - s0 + 1) * H]
-        w2_t = keep.tile([P, E * HP * 2 * N], U8, align_bytes=64, name="w2")
+        w2_t = [keep.tile([P, HP * 2 * N], U8, align_bytes=64, name="w2_%d" % e) for e in range(E)]
         w2_s = keep.tile([P, E * HP * N], U8, align_bytes=64, name="w2s")
         gate_t = keep.tile([P, E * C], F32, name="gate_t")
         xr_t = keep.tile([P, NB, T], F32, name="xr_t")
@@ -98,6 +98,12 @@ def tile_moe_res_mlp_gelu_kernel(
                 w1_words[e, s0:s1].bitcast(I32).rearrange("s p c -> p s c"),
             )
 
+        def load_w2(e):
+            nc.sync.dma_start(
+                w2_t[e][:].bitcast(I32).rearrange("p (g c) -> p g c", g=HP),
+                w2_words[e].bitcast(I32).rearrange("g p c -> p g c"),
+            )
+
         def load_scales1(i):
             e, s0, s1 = S1_LOADS[i]
             planes = s1_tiles[i][:].bitcast(I32).rearrange("p (s c) -> p s c", s=s1 - s0)
@@ -119,15 +125,13 @@ def tile_moe_res_mlp_gelu_kernel(
         load_w1(2)
         planes2 = w2_s[:].bitcast(I32).rearrange("p (g c) -> p g c", g=E * HP)
         rows2 = w2_scales.bitcast(I32).rearrange("e g (q r) c -> r q (e g) c", r=4)
-        nc.sync.dma_start(
-            w2_t[:].bitcast(I32).rearrange("p (g c) -> p g c", g=E * HP),
-            w2_words.bitcast(I32).rearrange("e g p c -> p (e g) c"),
-        )
+        load_w2(0)
         for r in range(4):
             nc.sync.dma_start(planes2[r:P:32], rows2[r])
         load_w1(3)
         load_scales1(2)
         nc.sync.dma_start(gate_t[:], gate[0:P, :])
+        load_w2(1)
         nc.sync.dma_start(xr_t[:], xr.rearrange("(m p) c -> p m c", p=P))
 
         def cast(eng, s, c0, c1):
@@ -228,11 +232,11 @@ def tile_moe_res_mlp_gelu_kernel(
         def mm2(t, m, y):
             e = t // 2
             for b in range(HP):
-                w0 = (e * HP + b) * N + m * P
+                w0 = b * N + m * P
                 nc.tensor.matmul_mx(
                     out=y,
-                    lhsT=w2_t[:, 2 * w0 : 2 * (w0 + P)].bitcast(FP4X4),
-                    lhsT_scale=w2_s[:, w0 : w0 + P],
+                    lhsT=w2_t[e][:, 2 * w0 : 2 * (w0 + P)].bitcast(FP4X4),
+                    lhsT_scale=w2_s[:, e * HP * N + w0 : e * HP * N + w0 + P],
                     rhs=h_words[t][:, b * P : (b + 1) * P].bitcast(FP8X4),
                     rhs_scale=h_bytes[t][:, b * P : (b + 1) * P],
                     start=(b == 0),
@@ -256,19 +260,19 @@ def tile_moe_res_mlp_gelu_kernel(
             idx = offsets[:, t * (P // 16) : (t + 1) * (P // 16)]
             nc.vector.tensor_tensor(win[m][:].indirect(idx), y_g[t, m], gate_t[:, t * P : (t + 1) * P], MULT)
 
-        def finish(m):
-            nc.vector.tensor_tensor(res[m][:], win[m][:], xr_t[:, m, :], mybir.AluOpType.add)
-            nc.sync.dma_start(out[m * P : (m + 1) * P, :], res[m][:])
+        def finish(m, c0=0, c1=T):
+            nc.vector.tensor_tensor(res[m][:, c0:c1], win[m][:, c0:c1], xr_t[:, m, c0:c1], mybir.AluOpType.add)
+            nc.sync.dma_start(out[m * P : (m + 1) * P, c0:c1], res[m][:, c0:c1])
 
         def last_block():
             m = NB - 1
             y = turn.tile([P, S - LATE, P], F32, name="y_last", offset=BANK * 7)
             for t in range(LATE, S):
                 mm2(t, m, y[:, t - LATE, :])
-            y_sb = keep.tile([P, (S - LATE) * P], F32, name="y_last_sb")
-            nc.scalar.copy(y_sb[:], y[:].rearrange("p t c -> p (t c)"))
-            nc.vector.tensor_tensor(win[m][:].indirect(offsets[:, LATE * P // 16 :]), y_sb[:], gate_t[:, LATE * P :], MULT)
-            finish(m)
+            y_sb = keep.tile([P, S - LATE, P], F32, name="y_last_sb")
+            nc.scalar.copy(y_sb[:], y[:])
+            for t in range(LATE, S):
+                y_g[t, m] = y_sb[:, t - LATE, :]
 
         PIECES = ((0, 3), (3, TB))
 
@@ -289,7 +293,7 @@ def tile_moe_res_mlp_gelu_kernel(
                 for j in range(j0, j1):
                     nc.tensor.transpose(acc[:, (j - j0) * P : (j - j0 + 1) * P], turned[:, j, :], ident[:])
                 nc.scalar.copy(res[m][:, j0 * P : j1 * P], acc[:, 0 : (j1 - j0) * P])
-                nc.sync.dma_start(out[m * P : (m + 1) * P, j0 * P : j1 * P], res[m][:, j0 * P : j1 * P])
+                nc.scalar.dma_start(out[m * P : (m + 1) * P, j0 * P : j1 * P], res[m][:, j0 * P : j1 * P])
 
         tokens(0)
         gather(0, 0, "gw00", "gb00")
@@ -335,6 +339,11 @@ def tile_moe_res_mlp_gelu_kernel(
         scatter(2, 1)
         scatter(3, 0)
         scatter(3, 1)
-        finish(1)
         last_block()
+        scatter(2, 2)
+        finish(1, 0, 384)
+        scatter(3, 2)
+        finish(1, 384, T)
+        finish(2, 0, 384)
+        finish(2, 384, T)
         turn_back(0, sum_turned(0))

@@ -63,7 +63,7 @@ def tile_moe_res_mlp_gelu_kernel(
                 w1_s[e, s] = tl[:, (s - s0) * H : (s - s0 + 1) * H]
         w2_t = [keep.tile([P, HP * 2 * N], U8, align_bytes=64, name="w2_%d" % e) for e in range(E)]
         w2_s = keep.tile([P, E * HP * N], U8, align_bytes=64, name="w2s")
-        gate_t = keep.tile([P, E * C], F32, name="gate_t")
+        gate_t = [keep.tile([P, C], F32, name="gate_t%d" % e) for e in range(E)]
         xr_t = keep.tile([P, NB, T], F32, name="xr_t")
         win = [keep.tile([P, T], F32, name="win_%d" % m) for m in range(NB)]
         res = [keep.tile([P, T], F32, name="res_%d" % m) for m in range(NB)]
@@ -128,9 +128,10 @@ def tile_moe_res_mlp_gelu_kernel(
         load_w2(0)
         for r in range(4):
             nc.sync.dma_start(planes2[r:P:32], rows2[r])
+        nc.sync.dma_start(gate_t[0][:], gate[0:P, 0:C])
         load_w1(3)
         load_scales1(2)
-        nc.sync.dma_start(gate_t[:], gate[0:P, :])
+        nc.sync.dma_start(gate_t[1][:], gate[0:P, C : 2 * C])
         load_w2(1)
         nc.sync.dma_start(xr_t[:], xr.rearrange("(m p) c -> p m c", p=P))
 
@@ -258,7 +259,7 @@ def tile_moe_res_mlp_gelu_kernel(
 
         def scatter(t, m):
             idx = offsets[:, t * (P // 16) : (t + 1) * (P // 16)]
-            nc.vector.tensor_tensor(win[m][:].indirect(idx), y_g[t, m], gate_t[:, t * P : (t + 1) * P], MULT)
+            nc.vector.tensor_tensor(win[m][:].indirect(idx), y_g[t, m], gate_t[t // 2][:, (t % 2) * P : (t % 2 + 1) * P], MULT)
 
         def finish(m, c0=0, c1=T):
             nc.vector.tensor_tensor(res[m][:, c0:c1], win[m][:, c0:c1], xr_t[:, m, c0:c1], mybir.AluOpType.add)
@@ -311,16 +312,17 @@ def tile_moe_res_mlp_gelu_kernel(
         layer2(0, 0, 1, 4)
         y_out(0, 0, 1, keep)
         layer2(0, 1, NB, 5)
-        y_out(0, 1, NB, keep)
         gather(1, 1, "x_bf2", "x_raw2")
         gather_last(2, relay, HG, HG + 4 * P)
         gather_last(3, relay, HG + H, HG + H + 4 * P)
+        scatter(0, 0)
         hidden(1)
+        y_out(0, 1, NB, relay, 4 * N)
         for b in range(HP):
             for s in range(KP):
                 mm1(2, s, (b,))
-        for m in range(NB):
-            scatter(0, m)
+        scatter(0, 1)
+        scatter(0, 2)
         hidden(2)
         layer2(1, 0, NB, 0)
         y_out(1, 0, 2, keep)

@@ -27,7 +27,7 @@ LATE = 2
 TB = T // P
 HG = 6 * 4 * N
 CASTS = (
-    (("v", 0, 256), ("v", 256, 512), ("s", 512, T)),
+    (("v", 0, 256), ("v", 256, 384), ("s", 384, 512), ("s", 512, T)),
     (("s", 0, 256), ("s", 256, 512), ("v", 512, T)),
     (("s", 0, 256), ("s", 256, 384), ("v", 384, 512), ("v", 512, 576), ("s", 576, T)),
 )
@@ -112,8 +112,8 @@ def tile_moe_res_mlp_gelu_kernel(
                 nc.sync.dma_start(planes[r:P:32], rows[r])
 
         CHUNKS = ((0, 256), (256, 512), (512, T))
-        load_x(0, 0, 256)
-        load_x(0, 256, T)
+        load_x(0, 0, 512)
+        load_x(0, 512, T)
         nc.sync.dma_start(offsets[:], offs)
         load_x(1, 0, T)
         load_scales1(0)

@@ -115,7 +115,8 @@ def tile_moe_res_mlp_gelu_kernel(
         load_x(0, 0, 512)
         load_x(0, 512, T)
         nc.sync.dma_start(offsets[:], offs)
-        load_x(1, 0, T)
+        load_x(1, 0, 512)
+        load_x(1, 512, T)
         load_scales1(0)
         load_w1(0)
         for c in CHUNKS:

@@ -23,13 +23,15 @@ HP = H // 512
 NB = N // P
 S = E * C // P
 BANK = 2048
-LATE = 2
-TB = T // P
-HG = 6 * 4 * N
+HG = 2 * H
+XB = 6 * HG
+PL = 5 * HG + 512
+XL = XB + (KP - 1) * 8 * T
+HW = XB + KP * 8 * T + H
 CASTS = (
-    (("v", 0, 256), ("v", 256, 384), ("s", 384, 512), ("s", 512, T)),
-    (("s", 0, 256), ("s", 256, 512), ("v", 512, T)),
-    (("s", 0, 256), ("s", 256, 384), ("v", 384, 512), ("v", 512, 576), ("s", 576, T)),
+    (("v", 0, 256), ("v", 256, 320), ("s", 320, 512), ("s", 512, T)),
+    (("v", 0, 256), ("s", 256, 512), ("s", 512, T)),
+    (("v", 0, 256), ("s", 256, 512), ("s", 512, T)),
 )
 
 
@@ -45,16 +47,20 @@ def tile_moe_res_mlp_gelu_kernel(
         offsets = keep.tile([P, E * C // 16], U16, name="offsets")
 
         x_raw = [keep.tile([P, 4, T], F32, align_bytes=64, name="x_raw%d" % s, tag="x_raw%d" % s) for s in range(KP)]
-        x_bf = [keep.tile([P, T, 4], BF16, align_bytes=64, name="x_bf%d" % s, tag="x_bf%d" % s) for s in range(KP)]
+        x_bf = [relay.tile([P, T, 4], BF16, align_bytes=64, name="x_bf%d" % s, offset=XB + s * 8 * T) for s in range(KP)]
         x_words = [keep.tile([P, T], U32, align_bytes=64, name="x_words%d" % s) for s in range(KP)]
         g_words, g_bytes = {}, {}
         x_bytes = [keep.tile([P, T], U8, align_bytes=64, name="x_bytes%d" % s) for s in range(KP)]
-        W1_LOADS = ((0, 0, 1), (0, 1, 2), (0, 2, 3), (1, 0, KP))
-        w1_tiles = [keep.tile([P, (s1 - s0) * 2 * H], U8, align_bytes=64, name="w1_%d_%d" % (e, s0)) for e, s0, s1 in W1_LOADS]
+        W1_LOADS = ((0, 0, 1, 0, HP), (0, 1, 2, 0, HP), (0, 2, 3, 0, HP), (1, 0, KP, 0, 1), (1, 0, KP, 1, HP))
+        w1_tiles = [
+            keep.tile([P, s1 - s0, (b1 - b0) * H], U8, align_bytes=64, name="w1_%d_%d_%d" % (e, s0, b0))
+            for e, s0, s1, b0, b1 in W1_LOADS
+        ]
         w1_t = {}
-        for tl, (e, s0, s1) in zip(w1_tiles, W1_LOADS):
+        for tl, (e, s0, s1, b0, b1) in zip(w1_tiles, W1_LOADS):
             for s in range(s0, s1):
-                w1_t[e, s] = (tl, (s - s0) * 2 * H)
+                for b in range(b0, b1):
+                    w1_t[e, s, b] = tl[:, s - s0, (b - b0) * H : (b - b0 + 1) * H]
         S1_LOADS = ((0, 0, 1), (0, 1, KP), (1, 0, KP))
         s1_tiles = [keep.tile([P, (s1 - s0) * H], U8, align_bytes=64, name="w1s_%d_%d" % (e, s0)) for e, s0, s1 in S1_LOADS]
         w1_s = {}
@@ -63,13 +69,15 @@ def tile_moe_res_mlp_gelu_kernel(
                 w1_s[e, s] = tl[:, (s - s0) * H : (s - s0 + 1) * H]
         w2_t = [keep.tile([P, HP * 2 * N], U8, align_bytes=64, name="w2_%d" % e) for e in range(E)]
         w2_s = keep.tile([P, E * HP * N], U8, align_bytes=64, name="w2s")
-        gate_t = [keep.tile([P, C], F32, name="gate_t%d" % e) for e in range(E)]
+        gate_col = keep.tile([P, S], F32, name="gate_col")
+        gate_all = keep.tile([P, E * C], F32, name="gate_all")
+        gate_t = [gate_all[:, e * C : (e + 1) * C] for e in range(E)]
         xr_t = keep.tile([P, NB, T], F32, name="xr_t")
         win = [keep.tile([P, T], F32, name="win_%d" % m) for m in range(NB)]
         res = [keep.tile([P, T], F32, name="res_%d" % m) for m in range(NB)]
-        h_bf, y_ps, y_g = {}, {}, {}
-        h_gr = [relay.tile([P, HP, P, 4], BF16, align_bytes=64, name="h_gr%d" % s, offset=HG + s * 2 * H) for s in range(S)]
-        h_words = [keep.tile([P, HP * P], U32, align_bytes=64, name="h_words%d" % s) for s in range(S)]
+        h_bf = {}
+        h_gr = [relay.tile([P, HP, P, 4], BF16, align_bytes=64, name="h_gr%d" % s, offset=s * HG) for s in range(S)]
+        h_words = {}
         h_bytes = [keep.tile([P, HP * P], U8, align_bytes=64, name="h_bytes%d" % s) for s in range(S)]
         ident = keep.tile([P, P], F32, name="ident")
         warm = keep.tile([P, 1], F32, name="warm")
@@ -92,10 +100,10 @@ def tile_moe_res_mlp_gelu_kernel(
             )
 
         def load_w1(i):
-            e, s0, s1 = W1_LOADS[i]
+            e, s0, s1, b0, b1 = W1_LOADS[i]
             nc.sync.dma_start(
-                w1_tiles[i][:].bitcast(I32).rearrange("p (s c) -> p s c", s=s1 - s0),
-                w1_words[e, s0:s1].bitcast(I32).rearrange("s p c -> p s c"),
+                w1_tiles[i][:].bitcast(I32),
+                w1_words[e, s0:s1, :, b0 * H : b1 * H].bitcast(I32).rearrange("s p c -> p s c"),
             )
 
         def load_w2(e):
@@ -112,27 +120,25 @@ def tile_moe_res_mlp_gelu_kernel(
                 nc.sync.dma_start(planes[r:P:32], rows[r])
 
         CHUNKS = ((0, 256), (256, 512), (512, T))
-        load_x(0, 0, 512)
-        load_x(0, 512, T)
+        load_x(0, 0, T)
         nc.sync.dma_start(offsets[:], offs)
-        load_x(1, 0, 512)
-        load_x(1, 512, T)
+        nc.sync.dma_start(gate_col[:], gate[0, :].rearrange("(p i) -> p i", i=S))
+        load_x(1, 0, T)
         load_scales1(0)
         load_w1(0)
-        for c in CHUNKS:
-            load_x(2, *c)
+        load_x(2, 0, 512)
+        load_x(2, 512, T)
         load_scales1(1)
         load_w1(1)
         load_w1(2)
+        load_scales1(2)
+        load_w1(3)
         planes2 = w2_s[:].bitcast(I32).rearrange("p (g c) -> p g c", g=E * HP)
         rows2 = w2_scales.bitcast(I32).rearrange("e g (q r) c -> r q (e g) c", r=4)
-        load_w2(0)
         for r in range(4):
             nc.sync.dma_start(planes2[r:P:32], rows2[r])
-        nc.sync.dma_start(gate_t[0][:], gate[0:P, 0:C])
-        load_w1(3)
-        load_scales1(2)
-        nc.sync.dma_start(gate_t[1][:], gate[0:P, C : 2 * C])
+        load_w2(0)
+        load_w1(4)
         load_w2(1)
         nc.sync.dma_start(xr_t[:], xr.rearrange("(m p) c -> p m c", p=P))
 
@@ -157,79 +163,82 @@ def tile_moe_res_mlp_gelu_kernel(
             for c in CHUNKS:
                 quant_x(s, *c)
 
-        def gather(s, e, words_tag=None, bytes_tag=None):
-            g_words[s, e] = keep.tile([P, C], U32, align_bytes=64, name="g_words%d_%d" % (s, e), tag=words_tag)
-            g_bytes[s, e] = keep.tile([P, C], U8, align_bytes=64, name="g_bytes%d_%d" % (s, e), tag=bytes_tag)
+        def gather(s, e, pool, place_words=None, place_bytes=None):
+            g_words[s, e] = pool.tile([P, C], U32, align_bytes=64, name="g_words%d_%d" % (s, e), offset=place_words)
+            g_bytes[s, e] = pool.tile([P, C], U8, align_bytes=64, name="g_bytes%d_%d" % (s, e), offset=place_bytes)
             idx = offsets[:, e * C // 16 : (e + 1) * C // 16]
             nc.vector.tensor_copy(g_words[s, e][:], x_words[s][:].indirect(idx))
             nc.vector.tensor_copy(g_bytes[s, e][:], x_bytes[s][:].indirect(idx))
 
         last = {}
 
-        def gather_last(t, pool, place_words=None, place_bytes=None):
-            words = pool.tile([P, P], U32, align_bytes=64, name="last_words%d" % t, offset=place_words)
-            plane = pool.tile([P, P], U8, align_bytes=64, name="last_bytes%d" % t, offset=place_bytes)
+        def gather_tile(s, t, pool, place_words=None, place_bytes=None):
+            words = pool.tile([P, P], U32, align_bytes=64, name="t_words%d_%d" % (s, t), offset=place_words)
+            plane = pool.tile([P, P], U8, align_bytes=64, name="t_bytes%d_%d" % (s, t), offset=place_bytes)
             idx = offsets[:, t * P // 16 : (t + 1) * P // 16]
-            nc.vector.tensor_copy(words[:], x_words[KP - 1][:].indirect(idx))
-            nc.vector.tensor_copy(plane[:], x_bytes[KP - 1][:].indirect(idx))
-            last[t] = (words[:], plane[:])
+            nc.vector.tensor_copy(words[:], x_words[s][:].indirect(idx))
+            nc.vector.tensor_copy(plane[:], x_bytes[s][:].indirect(idx))
+            last[s, t] = (words[:], plane[:])
 
         def operand(s, t):
-            if s == KP - 1:
-                return last[t]
+            if (s, t) in last:
+                return last[s, t]
             e, c0 = t // 2, (t % 2) * P
             return g_words[s, e][:, c0 : c0 + P], g_bytes[s, e][:, c0 : c0 + P]
 
         banks = {}
 
-        def mm1(t, s, halves=range(HP)):
+        def mm1(t, s, halves=range(HP), first=0, final=KP - 1):
             e = t // 2
             words, plane = operand(s, t)
             for b in halves:
-                if s == 0:
-                    banks[t, b] = turn.tile([P, 512], F32, name="acc%d_%d" % (t, b), offset=BANK * (2 * (t % 2) + b))
+                if s == first:
+                    banks[t, b] = turn.tile([P, 512], F32, name="acc%d_%d" % (t, b), offset=BANK * (2 * t + b))
                 nc.tensor.matmul_mx(
                     out=banks[t, b][:],
                     lhsT=words.bitcast(FP8X4),
                     lhsT_scale=plane,
-                    rhs=w1_t[e, s][0][:, w1_t[e, s][1] + b * 1024 : w1_t[e, s][1] + (b + 1) * 1024].bitcast(FP4X4),
+                    rhs=w1_t[e, s, b].bitcast(FP4X4),
                     rhs_scale=w1_s[e, s][:, b * 512 : (b + 1) * 512],
-                    start=(s == 0),
-                    stop=(s == KP - 1),
+                    start=(s == first),
+                    stop=(s == final),
                 )
 
-        def quant_h(t, b0, b1):
-            nc.vector.quantize_mx(
-                out=h_words[t][:, b0 * P : b1 * P].bitcast(FP8X4),
-                scales=h_bytes[t][:, b0 * P : b1 * P],
-                in_=h_gr[t][:, b0:b1].rearrange("p b c t -> p (b c t)"),
-            )
-
-        def hidden(t, engs="ss"):
+        def layer1(t, order):
             for b in range(HP):
-                if b == HP - 1:
-                    h_bf[t, b] = relay.tile([P, 512], BF16, align_bytes=64, name="h_bf%d_%d" % (t, b), offset=t * 4 * N)
+                for s in order:
+                    mm1(t, s, (b,), order[0], order[-1])
+
+        def gelu(t):
+            for b in range(HP):
+                if t == 2:
+                    h_bf[t, b] = relay.tile([P, 512], BF16, align_bytes=64, name="h_bf2_%d" % b, offset=(HW + 64 - H, HW + 704)[b])
+                elif (t, b) == (S - 1, HP - 1):
+                    h_bf[t, b] = relay.tile([P, 512], BF16, align_bytes=64, name="h_bf_last", offset=S * HG + 2 * P)
                 else:
-                    h_bf[t, b] = keep.tile([P, 512], BF16, align_bytes=64, name="h_bf%d_%d" % (t, b))
+                    h_bf[t, b] = keep.tile([P, 512], BF16, align_bytes=64, name="h_bf%d_%d" % (t, b), tag="held" if (t, b) in ((0, 1), (1, 0)) else "h_bf%d_%d" % (t, b))
                 nc.scalar.activation(
                     h_bf[t, b][:].rearrange("c (u p e) -> c u p e", u=2, e=2),
                     banks[t, b][:].rearrange("c (p u e) -> c u p e", u=2, e=2),
                     ACT.Gelu_apprx_tanh,
                 )
-                xt = turn.tile([P, 2, P], F32, name="xt%d_%d" % (t, b), offset=BANK * (4 + 2 * (t % 2) + b))
+
+        def turn_over(t, places):
+            for b in range(HP):
+                xt = turn.tile([P, 2, P], F32, name="xt%d_%d" % (t, b), offset=BANK * places[b])
                 pairs = h_bf[t, b][:].bitcast(F32)
                 for u in range(2):
                     nc.tensor.transpose(xt[:, u, :], pairs[:, u * P : (u + 1) * P], ident[:])
                 dst = h_gr[t][:, b].rearrange("p c t -> p (c t)").bitcast(F32).rearrange("p (c u) -> p c u", u=2)
-                source = xt[:].rearrange("p u c -> p c u")
-                if engs[b] == "s":
-                    nc.scalar.copy(dst, source)
-                else:
-                    nc.vector.tensor_copy(dst, source)
-                if t == 0:
-                    quant_h(t, b, b + 1)
-            if t > 0:
-                quant_h(t, 0, HP)
+                nc.scalar.copy(dst, xt[:].rearrange("p u c -> p c u"))
+
+        def quant_h(t, pool, place=None):
+            h_words[t] = pool.tile([P, HP * P], U32, align_bytes=64, name="h_words%d" % t, offset=place)
+            nc.vector.quantize_mx(
+                out=h_words[t][:].bitcast(FP8X4),
+                scales=h_bytes[t][:],
+                in_=h_gr[t][:].rearrange("p b c t -> p (b c t)"),
+            )
 
         def mm2(t, m, y):
             e = t // 2
@@ -245,108 +254,110 @@ def tile_moe_res_mlp_gelu_kernel(
                     stop=(b == HP - 1),
                 )
 
-        def layer2(t, m0, m1, bank):
-            y = turn.tile([P, m1 - m0, P], F32, name="y%d_%d" % (t, m0), offset=BANK * bank)
-            for m in range(m0, m1):
-                mm2(t, m, y[:, m - m0, :])
-                y_ps[t, m] = (y, m - m0)
+        def layer2(items, bank):
+            y = turn.tile([P, len(items), P], F32, name="y%d_%d" % items[0], offset=BANK * bank)
+            for i, (t, m) in enumerate(items):
+                mm2(t, m, y[:, i, :])
+            return y[:]
 
-        def y_out(t, m0, m1, pool, place=None):
-            y_sb = pool.tile([P, m1 - m0, P], F32, align_bytes=64, name="y_sb%d_%d" % (t, m0), offset=place)
-            y, i = y_ps[t, m0]
-            nc.scalar.copy(y_sb[:], y[:, i : i + m1 - m0, :])
-            for m in range(m0, m1):
-                y_g[t, m] = y_sb[:, m - m0, :]
+        gated = {}
 
-        def scatter(t, m):
-            idx = offsets[:, t * (P // 16) : (t + 1) * (P // 16)]
-            nc.vector.tensor_tensor(win[m][:].indirect(idx), y_g[t, m], gate_t[t // 2][:, (t % 2) * P : (t % 2 + 1) * P], MULT)
+        def weigh(items, y, pool, place=None):
+            n = len(items)
+            t0 = items[0][0]
+            z = pool.tile([P, n, P], F32, align_bytes=64, name="z%d_%d" % items[0], offset=place)
+            g = gate_t[t0 // 2]
+            if items[-1][0] == t0:
+                factor = g[:, (t0 % 2) * P : (t0 % 2 + 1) * P].unsqueeze(1).to_broadcast([P, n, P])
+            else:
+                factor = g.rearrange("p (i c) -> p i c", c=P)
+            nc.vector.tensor_tensor(z[:], y, factor, MULT)
+            for i, item in enumerate(items):
+                gated[item] = (z, i)
+
+        def scatter(eng, t0, t1, m):
+            z, i = gated[t0, m]
+            idx = offsets[:, t0 * (P // 16) : t1 * (P // 16)]
+            source = z[:, i : i + t1 - t0, :].rearrange("p i c -> p (i c)")
+            if eng == "v":
+                nc.vector.tensor_copy(win[m][:].indirect(idx), source)
+            else:
+                nc.scalar.activation(win[m][:].indirect(idx), source, ACT.Copy)
+
+        def carry(m, y):
+            z = relay.tile([P, P], F32, align_bytes=64, name="plain%d" % m, offset=PL + m * H)
+            nc.scalar.copy(z[:], y[:, 0, :])
+            return z
+
+        def scatter_gated(m, z):
+            nc.vector.tensor_tensor(win[m][:].indirect(offsets[:, 0 : P // 16]), z[:], gate_t[0][:, 0:P], MULT)
 
         def finish(m, c0=0, c1=T):
             nc.vector.tensor_tensor(res[m][:, c0:c1], win[m][:, c0:c1], xr_t[:, m, c0:c1], mybir.AluOpType.add)
             nc.sync.dma_start(out[m * P : (m + 1) * P, c0:c1], res[m][:, c0:c1])
 
-        def last_block():
-            m = NB - 1
-            y = turn.tile([P, S - LATE, P], F32, name="y_last", offset=BANK * 7)
-            for t in range(LATE, S):
-                mm2(t, m, y[:, t - LATE, :])
-            y_sb = keep.tile([P, S - LATE, P], F32, name="y_last_sb")
-            nc.scalar.copy(y_sb[:], y[:])
-            for t in range(LATE, S):
-                y_g[t, m] = y_sb[:, t - LATE, :]
-
-        PIECES = ((0, 3), (3, TB))
-
-        def sum_turned(m):
-            turned = keep.tile([P, TB, P], F32, name="turned%d" % m)
-            for i, (j0, j1) in enumerate(PIECES):
-                acc = turn.tile([P, 512], F32, name="sum%d" % i, offset=BANK * i)
-                for j in range(j0, j1):
-                    o = acc[:, (j - j0) * P : (j - j0 + 1) * P]
-                    nc.tensor.matmul(o, xr_t[:, m, j * P : (j + 1) * P], ident[:], start=True, stop=False, is_transpose=True)
-                    nc.tensor.matmul(o, win[m][:, j * P : (j + 1) * P], ident[:], start=False, stop=True, is_transpose=True)
-                nc.scalar.copy(turned[:, j0:j1, :].rearrange("p j c -> p (j c)"), acc[:, 0 : (j1 - j0) * P])
-            return turned
-
-        def turn_back(m, turned):
-            for i, (j0, j1) in enumerate(PIECES):
-                acc = turn.tile([P, 512], F32, name="back%d" % i, offset=BANK * (2 + i))
-                for j in range(j0, j1):
-                    nc.tensor.transpose(acc[:, (j - j0) * P : (j - j0 + 1) * P], turned[:, j, :], ident[:])
-                nc.scalar.copy(res[m][:, j0 * P : j1 * P], acc[:, 0 : (j1 - j0) * P])
-                nc.scalar.dma_start(out[m * P : (m + 1) * P, j0 * P : j1 * P], res[m][:, j0 * P : j1 * P])
-
         tokens(0)
-        gather(0, 0, "gw00", "gb00")
-        gather(0, 1, "gw01", "gb01")
+        spread = turn.tile([P, S, P], F32, name="spread", offset=BANK * 7)
+        for i in range(S):
+            nc.tensor.transpose(spread[:, i, :], gate_col[:, i : i + 1].to_broadcast([P, P]), ident[:])
+        nc.scalar.copy(gate_all[:].rearrange("q (p i) -> q p i", i=S), spread[:].rearrange("q i p -> q p i"))
+        gather(0, 0, keep)
         tokens(1)
-        gather(1, 0, "gw10", "gb10")
+        gather(1, 0, keep)
         for t in range(2):
             mm1(t, 0)
         tokens(2)
         for t in range(2):
-            gather_last(t, keep)
+            gather_tile(2, t, keep)
             mm1(t, 1)
             mm1(t, 2)
-        hidden(0, "vv")
-        layer2(0, 0, 1, 4)
-        y_out(0, 0, 1, keep)
-        layer2(0, 1, NB, 5)
-        gather(1, 1, "x_bf2", "x_raw2")
-        gather_last(2, relay, HG, HG + 4 * P)
-        gather_last(3, relay, HG + H, HG + H + 4 * P)
-        scatter(0, 0)
-        hidden(1)
-        y_out(0, 1, NB, relay, 4 * N)
-        for b in range(HP):
-            for s in range(KP):
-                mm1(2, s, (b,))
-        scatter(0, 1)
-        scatter(0, 2)
-        hidden(2)
-        layer2(1, 0, NB, 0)
-        y_out(1, 0, 2, keep)
-        y_out(1, 2, NB, relay, 2 * 4 * N)
-        for b in range(HP):
-            for s in range(KP):
-                mm1(3, s, (b,))
-        for m in range(NB):
-            scatter(1, m)
-        hidden(3)
-        layer2(2, 0, NB - 1, 6)
-        y_out(2, 0, NB - 1, relay, 3 * 4 * N)
-        layer2(3, 0, NB - 1, 5)
-        y_out(3, 0, NB - 1, keep)
-        scatter(2, 0)
-        scatter(2, 1)
-        scatter(3, 0)
-        scatter(3, 1)
-        last_block()
-        scatter(2, 2)
+        gather(0, 1, relay, XL, XL + 4 * C)
+        gather_tile(1, 2, relay, XL + 5 * C, XL + 5 * C + 4 * P)
+        gather_tile(2, 2, keep)
+        gelu(0)
+        turn_over(0, (0, 1))
+        quant_h(0, relay, HW)
+        gather_tile(1, 3, relay, 0, 4 * P)
+        y00 = layer2([(0, 0)], 0)
+        y01 = layer2([(0, 1)], 1)
+        gelu(1)
+        y02 = layer2([(0, 2)], 2)
+        gather_tile(2, 3, relay, HW + 192, HW + 64)
+        scatter_gated(0, carry(0, y00))
+        z01 = carry(1, y01)
+        turn_over(1, (0, 1))
+        quant_h(1, relay, PL + 64 - H)
+        scatter_gated(1, z01)
+        weigh([(0, 2)], y02, relay, HG)
+        scatter("v", 0, 1, 2)
+        layer1(2, (0, 1, 2))
+        gelu(2)
+        turn_over(2, (4, 5))
+        layer1(3, (2, 0, 1))
+        second = [(1, m) for m in range(NB)]
+        y1 = layer2(second, 4)
+        quant_h(2, keep)
+        weigh(second[:1], y1[:, 0:1, :], relay, 2 * HG)
+        scatter("v", 1, 2, 0)
+        gelu(3)
+        third = [(2, m) for m in range(NB)]
+        turn_over(3, (6, 7))
+        y2 = layer2(third, 6)
+        weigh(second[1:], y1[:, 1:NB, :], relay, S * HG)
+        scatter("s", 1, 2, 2)
+        scatter("s", 1, 2, 1)
+        quant_h(3, keep)
+        weigh(third, y2, relay, 3 * HG)
+        scatter("v", 2, 3, 0)
+        fourth = [(3, m) for m in range(NB)]
+        y3 = layer2(fourth, 3)
+        weigh(fourth, y3, keep)
+        scatter("s", 2, 3, 2)
+        scatter("v", 3, 4, 0)
+        scatter("s", 3, 4, 2)
+        scatter("s", 2, 3, 1)
+        scatter("s", 3, 4, 1)
+        finish(0)
+        finish(2)
         finish(1, 0, 384)
-        scatter(3, 2)
         finish(1, 384, T)
-        finish(2, 0, 384)
-        finish(2, 384, T)
-        turn_back(0, sum_turned(0))

@@ -17,22 +17,17 @@ FP8X4 = mybir.dt.float8_e4m3fn_x4
 FP4X4 = mybir.dt.float4_e2m1fn_x4
 ACT = mybir.ActivationFunctionType
 MULT = mybir.AluOpType.mult
+ADD = mybir.AluOpType.add
 
 KP = K // 512
 HP = H // 512
 NB = N // P
 S = E * C // P
 BANK = 2048
+ROUNDED = 8 * P
 HG = 2 * H
-XB = 6 * HG
-PL = 5 * HG + 512
-XL = XB + (KP - 1) * 8 * T
-HW = XB + KP * 8 * T + H
-CASTS = (
-    (("v", 0, 256), ("v", 256, 320), ("s", 320, 512), ("s", 512, T)),
-    (("v", 0, 256), ("s", 256, 512), ("s", 512, T)),
-    (("v", 0, 256), ("s", 256, 512), ("s", 512, T)),
-)
+ROW13 = 10 * ROUNDED
+LAST_H = S * HG
 
 
 def tile_moe_res_mlp_gelu_kernel(
@@ -42,68 +37,63 @@ def tile_moe_res_mlp_gelu_kernel(
     with ExitStack() as ctx:
         keep = ctx.enter_context(tc.tile_pool(name="keep", bufs=1))
         turn = ctx.enter_context(tc.psum_pool(name="turn", bufs=1))
+        stage = ctx.enter_context(tc.tile_pool(name="stage", bufs=1))
         relay = ctx.enter_context(tc.tile_pool(name="relay", bufs=1))
 
         offsets = keep.tile([P, E * C // 16], U16, name="offsets")
-
-        x_raw = [keep.tile([P, 4, T], F32, align_bytes=64, name="x_raw%d" % s, tag="x_raw%d" % s) for s in range(KP)]
-        x_bf = [relay.tile([P, T, 4], BF16, align_bytes=64, name="x_bf%d" % s, offset=XB + s * 8 * T) for s in range(KP)]
-        x_words = [keep.tile([P, T], U32, align_bytes=64, name="x_words%d" % s) for s in range(KP)]
-        g_words, g_bytes = {}, {}
-        x_bytes = [keep.tile([P, T], U8, align_bytes=64, name="x_bytes%d" % s) for s in range(KP)]
-        W1_LOADS = ((0, 0, 1, 0, HP), (0, 1, 2, 0, HP), (0, 2, 3, 0, HP), (1, 0, KP, 0, 1), (1, 0, KP, 1, HP))
-        w1_tiles = [
-            keep.tile([P, s1 - s0, (b1 - b0) * H], U8, align_bytes=64, name="w1_%d_%d_%d" % (e, s0, b0))
-            for e, s0, s1, b0, b1 in W1_LOADS
-        ]
+        x_row = {
+            (s, j): keep.tile([P, T], F32, align_bytes=64, name="x%d_%d" % (s, j))
+            for s in range(KP)
+            for j in range(4)
+            if (s, j) != (1, 3)
+        }
+        x_row[1, 3] = stage.tile([P, T], F32, align_bytes=64, name="x1_3", offset=ROW13)
+        picked = {
+            (s, e): keep.tile([P, 4, C], F32, align_bytes=64, name="picked%d_%d" % (s, e))
+            for s in range(KP)
+            for e in range(E)
+            if (s, e) != (KP - 1, 0)
+        }
+        w1_by_pass = [keep.tile([P, HP, H], U8, align_bytes=64, name="w1_pass%d" % s) for s in range(KP)]
+        w1_by_half = [keep.tile([P, KP, H], U8, align_bytes=64, name="w1_half%d" % b) for b in range(HP)]
         w1_t = {}
-        for tl, (e, s0, s1, b0, b1) in zip(w1_tiles, W1_LOADS):
-            for s in range(s0, s1):
-                for b in range(b0, b1):
-                    w1_t[e, s, b] = tl[:, s - s0, (b - b0) * H : (b - b0 + 1) * H]
-        S1_LOADS = ((0, 0, 1), (0, 1, KP), (1, 0, KP))
-        s1_tiles = [keep.tile([P, (s1 - s0) * H], U8, align_bytes=64, name="w1s_%d_%d" % (e, s0)) for e, s0, s1 in S1_LOADS]
-        w1_s = {}
-        for tl, (e, s0, s1) in zip(s1_tiles, S1_LOADS):
-            for s in range(s0, s1):
-                w1_s[e, s] = tl[:, (s - s0) * H : (s - s0 + 1) * H]
+        for s in range(KP):
+            for b in range(HP):
+                w1_t[0, s, b] = w1_by_pass[s][:, b, :]
+                w1_t[1, s, b] = w1_by_half[b][:, s, :]
+        w1_s = [keep.tile([P, KP * H], U8, align_bytes=64, name="w1s_%d" % e) for e in range(E)]
         w2_t = [keep.tile([P, HP * 2 * N], U8, align_bytes=64, name="w2_%d" % e) for e in range(E)]
         w2_s = keep.tile([P, E * HP * N], U8, align_bytes=64, name="w2s")
-        gate_col = keep.tile([P, S], F32, name="gate_col")
         gate_all = keep.tile([P, E * C], F32, name="gate_all")
-        gate_t = [gate_all[:, e * C : (e + 1) * C] for e in range(E)]
         xr_t = keep.tile([P, NB, T], F32, name="xr_t")
-        win = [keep.tile([P, T], F32, name="win_%d" % m) for m in range(NB)]
+        win = [keep.tile([P, T], F32, name="win_%d" % m) for m in range(NB - 1)]
         res = [keep.tile([P, T], F32, name="res_%d" % m) for m in range(NB)]
-        h_bf = {}
-        h_gr = [relay.tile([P, HP, P, 4], BF16, align_bytes=64, name="h_gr%d" % s, offset=s * HG) for s in range(S)]
-        h_words = {}
-        h_bytes = [keep.tile([P, HP * P], U8, align_bytes=64, name="h_bytes%d" % s) for s in range(S)]
+        h_gr = [relay.tile([P, HP, P, 4], BF16, align_bytes=64, name="h_gr%d" % t, offset=t * HG) for t in range(S)]
+        h_words = [keep.tile([P, HP * P], U32, align_bytes=64, name="h_words%d" % t) for t in range(S)]
+        h_bytes = [keep.tile([P, HP * P], U8, align_bytes=64, name="h_bytes%d" % t) for t in range(S)]
         ident = keep.tile([P, P], F32, name="ident")
         warm = keep.tile([P, 1], F32, name="warm")
 
         nc.vector.memset(warm[:], 0.0)
         nc.scalar.activation(warm[:], warm[:], ACT.Gelu_apprx_tanh)
-        for tl in s1_tiles:
+        for tl in w1_s:
             nc.vector.memset(tl[:].bitcast(I32), 0)
         nc.vector.memset(w2_s[:].bitcast(I32), 0)
-        for plane in x_bytes:
-            nc.gpsimd.memset(plane[:].bitcast(I32), 0)
         make_identity(nc, ident[:])
-        for m in range(NB):
-            nc.gpsimd.memset(win[m][:], 0.0)
+        for tl in win:
+            nc.gpsimd.memset(tl[:], 0.0)
 
-        def load_x(s, c0, c1):
-            nc.sync.dma_start(
-                x_raw[s][:, :, c0:c1],
-                xT[512 * s : 512 * (s + 1), :].rearrange("(p j) w -> p j w", j=4)[:, :, c0:c1],
-            )
+        def load_x(s, j):
+            rows = xT[512 * s : 512 * (s + 1), :].rearrange("(p j) w -> p j w", j=4)
+            nc.sync.dma_start(x_row[s, j][:], rows[:, j, :])
 
-        def load_w1(i):
-            e, s0, s1, b0, b1 = W1_LOADS[i]
+        def load_w1_pass(s):
+            nc.sync.dma_start(w1_by_pass[s][:].rearrange("p b c -> p (b c)").bitcast(I32), w1_words[0, s].bitcast(I32))
+
+        def load_w1_half(b):
             nc.sync.dma_start(
-                w1_tiles[i][:].bitcast(I32),
-                w1_words[e, s0:s1, :, b0 * H : b1 * H].bitcast(I32).rearrange("s p c -> p s c"),
+                w1_by_half[b][:].bitcast(I32),
+                w1_words[1, :, :, b * H : (b + 1) * H].bitcast(I32).rearrange("s p c -> p s c"),
             )
 
         def load_w2(e):
@@ -112,252 +102,248 @@ def tile_moe_res_mlp_gelu_kernel(
                 w2_words[e].bitcast(I32).rearrange("g p c -> p g c"),
             )
 
-        def load_scales1(i):
-            e, s0, s1 = S1_LOADS[i]
-            planes = s1_tiles[i][:].bitcast(I32).rearrange("p (s c) -> p s c", s=s1 - s0)
-            rows = w1_scales[e, s0:s1].bitcast(I32).rearrange("s (q r) c -> r q s c", r=4)
+        def load_scales(planes, rows):
             for r in range(4):
                 nc.sync.dma_start(planes[r:P:32], rows[r])
 
-        CHUNKS = ((0, 256), (256, 512), (512, T))
-        load_x(0, 0, T)
+        def load_scales1(e):
+            planes = w1_s[e][:].bitcast(I32).rearrange("p (s c) -> p s c", s=KP)
+            load_scales(planes, w1_scales[e].bitcast(I32).rearrange("s (q r) c -> r q s c", r=4))
+
+        load_x(0, 0)
         nc.sync.dma_start(offsets[:], offs)
-        nc.sync.dma_start(gate_col[:], gate[0, :].rearrange("(p i) -> p i", i=S))
-        load_x(1, 0, T)
+        for i in range(1, 8):
+            load_x(i // 4, i % 4)
         load_scales1(0)
-        load_w1(0)
-        load_x(2, 0, 512)
-        load_x(2, 512, T)
+        load_w1_pass(1)
+        load_x(2, 0)
+        load_x(2, 1)
+        load_scales(
+            w2_s[:].bitcast(I32).rearrange("p (g c) -> p g c", g=E * HP),
+            w2_scales.bitcast(I32).rearrange("e g (q r) c -> r q (e g) c", r=4),
+        )
+        load_x(2, 2)
+        load_x(2, 3)
+        load_w1_pass(0)
         load_scales1(1)
-        load_w1(1)
-        load_w1(2)
-        load_scales1(2)
-        load_w1(3)
-        planes2 = w2_s[:].bitcast(I32).rearrange("p (g c) -> p g c", g=E * HP)
-        rows2 = w2_scales.bitcast(I32).rearrange("e g (q r) c -> r q (e g) c", r=4)
-        for r in range(4):
-            nc.sync.dma_start(planes2[r:P:32], rows2[r])
+        load_w1_pass(2)
+        load_w1_half(0)
+        load_w1_half(1)
         load_w2(0)
-        load_w1(4)
+        nc.sync.dma_start(gate_all[:], gate[0:P, :])
         load_w2(1)
         nc.sync.dma_start(xr_t[:], xr.rearrange("(m p) c -> p m c", p=P))
 
-        def cast(eng, s, c0, c1):
-            dst = x_bf[s][:, c0:c1, :].rearrange("p (c i) t -> p c t i", i=4)
-            source = x_raw[s][:, :, c0:c1].rearrange("p t (c i) -> p c t i", i=4)
+        def gather(eng, s, j, t0, t1):
+            e, c0 = t0 // 2, (t0 % 2) * P
+            dst = picked[s, e][:, j, c0 : c0 + (t1 - t0) * P]
+            source = x_row[s, j][:].indirect(offsets[:, t0 * P // 16 : t1 * P // 16])
             if eng == "v":
                 nc.vector.tensor_copy(dst, source)
             else:
                 nc.scalar.activation(dst, source, ACT.Copy)
 
-        def quant_x(s, c0, c1):
-            nc.vector.quantize_mx(
-                out=x_words[s][:, c0:c1].bitcast(FP8X4),
-                scales=x_bytes[s][:, c0:c1],
-                in_=x_bf[s][:, c0:c1, :].rearrange("p c t -> p (c t)"),
-            )
+        rounded, codes = {}, {}
 
-        def tokens(s):
-            for eng, c0, c1 in CASTS[s]:
-                cast(eng, s, c0, c1)
-            for c in CHUNKS:
-                quant_x(s, *c)
+        def gather_rounded(s, j, t0, t1):
+            tl = rounded[s, 0][0]
+            idx = offsets[:, t0 * P // 16 : t1 * P // 16]
+            nc.vector.tensor_copy(tl[:, t0 * P : t1 * P, j], x_row[s, j][:].indirect(idx))
 
-        def gather(s, e, pool, place_words=None, place_bytes=None):
-            g_words[s, e] = pool.tile([P, C], U32, align_bytes=64, name="g_words%d_%d" % (s, e), offset=place_words)
-            g_bytes[s, e] = pool.tile([P, C], U8, align_bytes=64, name="g_bytes%d_%d" % (s, e), offset=place_bytes)
-            idx = offsets[:, e * C // 16 : (e + 1) * C // 16]
-            nc.vector.tensor_copy(g_words[s, e][:], x_words[s][:].indirect(idx))
-            nc.vector.tensor_copy(g_bytes[s, e][:], x_bytes[s][:].indirect(idx))
+        def weave(eng, s, t0, t1, place):
+            e, c0, n = t0 // 2, (t0 % 2) * P, (t1 - t0) * P
+            tl = stage.tile([P, n, 4], BF16, align_bytes=64, name="rounded%d_%d" % (s, t0), offset=place * ROUNDED)
+            source = picked[s, e][:, :, c0 : c0 + n]
+            if eng == "g":
+                nc.gpsimd.tensor_copy(tl[:], source.rearrange("p t c -> p c t"))
+            else:
+                dst, source = tl[:].rearrange("p (c i) t -> p c t i", i=4), source.rearrange("p t (c i) -> p c t i", i=4)
+                if eng == "v":
+                    nc.vector.tensor_copy(dst, source)
+                else:
+                    nc.scalar.activation(dst, source, ACT.Copy)
+            rounded[s, t0] = (tl, t1)
 
-        last = {}
+        def quant_x(s, t0, pool, place=None):
+            tl, t1 = rounded[s, t0]
+            tl = tl[:, 0 : (t1 - t0) * P, :]
+            words = pool.tile([P, (t1 - t0) * P], U32, align_bytes=64, name="x_words%d_%d" % (s, t0), offset=place)
+            plane = keep.tile([P, (t1 - t0) * P], U8, align_bytes=64, name="x_bytes%d_%d" % (s, t0))
+            nc.vector.quantize_mx(out=words[:].bitcast(FP8X4), scales=plane[:], in_=tl.rearrange("p c t -> p (c t)"))
+            for t in range(t0, t1):
+                codes[s, t] = (words[:, (t - t0) * P : (t - t0 + 1) * P], plane[:, (t - t0) * P : (t - t0 + 1) * P])
 
-        def gather_tile(s, t, pool, place_words=None, place_bytes=None):
-            words = pool.tile([P, P], U32, align_bytes=64, name="t_words%d_%d" % (s, t), offset=place_words)
-            plane = pool.tile([P, P], U8, align_bytes=64, name="t_bytes%d_%d" % (s, t), offset=place_bytes)
-            idx = offsets[:, t * P // 16 : (t + 1) * P // 16]
-            nc.vector.tensor_copy(words[:], x_words[s][:].indirect(idx))
-            nc.vector.tensor_copy(plane[:], x_bytes[s][:].indirect(idx))
-            last[s, t] = (words[:], plane[:])
+        banks, h_bf = {}, {}
+        first = (1, 0)
 
-        def operand(s, t):
-            if (s, t) in last:
-                return last[s, t]
-            e, c0 = t // 2, (t % 2) * P
-            return g_words[s, e][:, c0 : c0 + P], g_bytes[s, e][:, c0 : c0 + P]
-
-        banks = {}
-
-        def mm1(t, s, halves=range(HP), first=0, final=KP - 1):
+        def layer1(t, b, passes=range(KP)):
             e = t // 2
-            words, plane = operand(s, t)
-            for b in halves:
-                if s == first:
+            for s in passes:
+                if s == first[e]:
                     banks[t, b] = turn.tile([P, 512], F32, name="acc%d_%d" % (t, b), offset=BANK * (2 * t + b))
+                words, plane = codes[s, t]
                 nc.tensor.matmul_mx(
                     out=banks[t, b][:],
                     lhsT=words.bitcast(FP8X4),
                     lhsT_scale=plane,
                     rhs=w1_t[e, s, b].bitcast(FP4X4),
-                    rhs_scale=w1_s[e, s][:, b * 512 : (b + 1) * 512],
-                    start=(s == first),
-                    stop=(s == final),
+                    rhs_scale=w1_s[e][:, s * H + b * 512 : s * H + (b + 1) * 512],
+                    start=(s == first[e]),
+                    stop=(s == KP - 1),
                 )
 
-        def layer1(t, order):
-            for b in range(HP):
-                for s in order:
-                    mm1(t, s, (b,), order[0], order[-1])
-
-        def gelu(t):
-            for b in range(HP):
-                if t == 2:
-                    h_bf[t, b] = relay.tile([P, 512], BF16, align_bytes=64, name="h_bf2_%d" % b, offset=(HW + 64 - H, HW + 704)[b])
-                elif (t, b) == (S - 1, HP - 1):
-                    h_bf[t, b] = relay.tile([P, 512], BF16, align_bytes=64, name="h_bf_last", offset=S * HG + 2 * P)
-                else:
-                    h_bf[t, b] = keep.tile([P, 512], BF16, align_bytes=64, name="h_bf%d_%d" % (t, b), tag="held" if (t, b) in ((0, 1), (1, 0)) else "h_bf%d_%d" % (t, b))
-                nc.scalar.activation(
-                    h_bf[t, b][:].rearrange("c (u p e) -> c u p e", u=2, e=2),
-                    banks[t, b][:].rearrange("c (p u e) -> c u p e", u=2, e=2),
-                    ACT.Gelu_apprx_tanh,
-                )
-
-        def turn_over(t, places):
-            for b in range(HP):
-                xt = turn.tile([P, 2, P], F32, name="xt%d_%d" % (t, b), offset=BANK * places[b])
-                pairs = h_bf[t, b][:].bitcast(F32)
-                for u in range(2):
-                    nc.tensor.transpose(xt[:, u, :], pairs[:, u * P : (u + 1) * P], ident[:])
-                dst = h_gr[t][:, b].rearrange("p c t -> p (c t)").bitcast(F32).rearrange("p (c u) -> p c u", u=2)
-                nc.scalar.copy(dst, xt[:].rearrange("p u c -> p c u"))
-
-        def quant_h(t, pool, place=None):
-            h_words[t] = pool.tile([P, HP * P], U32, align_bytes=64, name="h_words%d" % t, offset=place)
-            nc.vector.quantize_mx(
-                out=h_words[t][:].bitcast(FP8X4),
-                scales=h_bytes[t][:],
-                in_=h_gr[t][:].rearrange("p b c t -> p (b c t)"),
+        def gelu(t, b, pool, place=None):
+            h_bf[t, b] = pool.tile([P, 512], BF16, align_bytes=64, name="h_bf%d_%d" % (t, b), offset=place)
+            nc.scalar.activation(
+                h_bf[t, b][:].rearrange("c (u p e) -> c u p e", u=2, e=2),
+                banks[t, b][:].rearrange("c (p u e) -> c u p e", u=2, e=2),
+                ACT.Gelu_apprx_tanh,
             )
 
-        def mm2(t, m, y):
-            e = t // 2
-            for b in range(HP):
-                w0 = b * N + m * P
-                nc.tensor.matmul_mx(
-                    out=y,
-                    lhsT=w2_t[e][:, 2 * w0 : 2 * (w0 + P)].bitcast(FP4X4),
-                    lhsT_scale=w2_s[:, e * HP * N + w0 : e * HP * N + w0 + P],
-                    rhs=h_words[t][:, b * P : (b + 1) * P].bitcast(FP8X4),
-                    rhs_scale=h_bytes[t][:, b * P : (b + 1) * P],
-                    start=(b == 0),
-                    stop=(b == HP - 1),
-                )
+        def turn_over(eng, t, b, bank):
+            xt = turn.tile([P, 2, P], F32, name="xt%d_%d" % (t, b), offset=BANK * bank)
+            pairs = h_bf[t, b][:].bitcast(F32)
+            for u in range(2):
+                nc.tensor.transpose(xt[:, u, :], pairs[:, u * P : (u + 1) * P], ident[:])
+            dst = h_gr[t][:, b].rearrange("p c t -> p (c t)").bitcast(F32).rearrange("p (c u) -> p c u", u=2)
+            if eng == "v":
+                nc.vector.tensor_copy(dst, xt[:].rearrange("p u c -> p c u"))
+            else:
+                nc.scalar.copy(dst, xt[:].rearrange("p u c -> p c u"))
+
+        def quant_h(t, b0=0, b1=HP):
+            nc.vector.quantize_mx(
+                out=h_words[t][:, b0 * P : b1 * P].bitcast(FP8X4),
+                scales=h_bytes[t][:, b0 * P : b1 * P],
+                in_=h_gr[t][:, b0:b1].rearrange("p b c t -> p (b c t)"),
+            )
+
+        y = {}
 
         def layer2(items, bank):
-            y = turn.tile([P, len(items), P], F32, name="y%d_%d" % items[0], offset=BANK * bank)
+            sums = turn.tile([P, len(items), P], F32, name="y%d_%d" % items[0], offset=BANK * bank)
             for i, (t, m) in enumerate(items):
-                mm2(t, m, y[:, i, :])
-            return y[:]
+                e = t // 2
+                y[t, m] = (sums, i)
+                for b in range(HP):
+                    w0 = b * N + m * P
+                    nc.tensor.matmul_mx(
+                        out=sums[:, i, :],
+                        lhsT=w2_t[e][:, 2 * w0 : 2 * (w0 + P)].bitcast(FP4X4),
+                        lhsT_scale=w2_s[:, e * HP * N + w0 : e * HP * N + w0 + P],
+                        rhs=h_words[t][:, b * P : (b + 1) * P].bitcast(FP8X4),
+                        rhs_scale=h_bytes[t][:, b * P : (b + 1) * P],
+                        start=(b == 0),
+                        stop=(b == HP - 1),
+                    )
 
         gated = {}
 
-        def weigh(items, y, pool, place=None):
-            n = len(items)
-            t0 = items[0][0]
-            z = pool.tile([P, n, P], F32, align_bytes=64, name="z%d_%d" % items[0], offset=place)
-            g = gate_t[t0 // 2]
-            if items[-1][0] == t0:
-                factor = g[:, (t0 % 2) * P : (t0 % 2 + 1) * P].unsqueeze(1).to_broadcast([P, n, P])
-            else:
-                factor = g.rearrange("p (i c) -> p i c", c=P)
-            nc.vector.tensor_tensor(z[:], y, factor, MULT)
-            for i, item in enumerate(items):
-                gated[item] = (z, i)
+        def weigh(t, blocks, pool, place=None):
+            n = len(blocks)
+            z = pool.tile([P, n, P], F32, align_bytes=64, name="z%d_%d" % (t, blocks[0]), offset=place)
+            factor = gate_all[:, t * P : (t + 1) * P].unsqueeze(1).to_broadcast([P, n, P])
+            sums, i = y[t, blocks[0]]
+            nc.vector.tensor_tensor(z[:], sums[:, i : i + n, :], factor, MULT)
+            for k, m in enumerate(blocks):
+                gated[t, m] = z[:, k, :]
 
-        def scatter(eng, t0, t1, m):
-            z, i = gated[t0, m]
-            idx = offsets[:, t0 * (P // 16) : t1 * (P // 16)]
-            source = z[:, i : i + t1 - t0, :].rearrange("p i c -> p (i c)")
+        def scatter(eng, t, m):
+            idx = offsets[:, t * (P // 16) : (t + 1) * (P // 16)]
             if eng == "v":
-                nc.vector.tensor_copy(win[m][:].indirect(idx), source)
+                nc.vector.tensor_copy(win[m][:].indirect(idx), gated[t, m])
             else:
-                nc.scalar.activation(win[m][:].indirect(idx), source, ACT.Copy)
+                nc.scalar.activation(win[m][:].indirect(idx), gated[t, m], ACT.Copy)
 
-        def carry(m, y):
-            z = relay.tile([P, P], F32, align_bytes=64, name="plain%d" % m, offset=PL + m * H)
-            nc.scalar.copy(z[:], y[:, 0, :])
-            return z
-
-        def scatter_gated(m, z):
-            nc.vector.tensor_tensor(win[m][:].indirect(offsets[:, 0 : P // 16]), z[:], gate_t[0][:, 0:P], MULT)
-
-        def finish(m, c0=0, c1=T):
-            nc.vector.tensor_tensor(res[m][:, c0:c1], win[m][:, c0:c1], xr_t[:, m, c0:c1], mybir.AluOpType.add)
+        def finish(eng, m, c0=0, c1=T):
+            eng.tensor_tensor(res[m][:, c0:c1], win[m][:, c0:c1], xr_t[:, m, c0:c1], ADD)
             nc.sync.dma_start(out[m * P : (m + 1) * P, c0:c1], res[m][:, c0:c1])
 
-        tokens(0)
-        spread = turn.tile([P, S, P], F32, name="spread", offset=BANK * 7)
-        for i in range(S):
-            nc.tensor.transpose(spread[:, i, :], gate_col[:, i : i + 1].to_broadcast([P, P]), ident[:])
-        nc.scalar.copy(gate_all[:].rearrange("q (p i) -> q p i", i=S), spread[:].rearrange("q i p -> q p i"))
-        gather(0, 0, keep)
-        tokens(1)
-        gather(1, 0, keep)
+        for j in range(4):
+            gather("v", 0, j, 0, 2)
+            gather("s", 0, j, 2, 4)
+        weave("g", 0, 0, 2, 6)
+        weave("g", 0, 2, 4, 8)
+        for j in range(4):
+            gather("v", 1, j, 0, 2)
+            gather("s", 1, j, 2, 4)
+        weave("v", 1, 0, 2, 13)
+        weave("s", 1, 2, 4, 15)
+        quant_x(0, 0, stage, ROW13)
+        quant_x(1, 0, keep)
+        for s in (1, 0):
+            for t in range(2):
+                for b in range(HP):
+                    layer1(t, b, (s,))
+        last = stage.tile([P, C, 4], BF16, align_bytes=64, name="rounded_last", offset=ROUNDED)
+        rounded[2, 0] = (last, 1)
+        rounded[2, 1] = (last[:, P:C, :], 2)
+        for j in range(3):
+            gather_rounded(2, j, 0, 2)
+            gather("s", 2, j, 2, 4)
+        gather_rounded(2, 3, 0, 1)
+        gather_rounded(2, 3, 1, 2)
+        gather("s", 2, 3, 2, 4)
+        quant_x(2, 0, keep)
+        quant_x(2, 1, keep)
+        weave("s", 2, 2, 4, 3)
+        quant_x(0, 2, stage, ROUNDED // 2)
+        quant_x(1, 2, stage, ROUNDED // 2 + 4 * C)
+        quant_x(2, 2, keep)
+
         for t in range(2):
-            mm1(t, 0)
-        tokens(2)
-        for t in range(2):
-            gather_tile(2, t, keep)
-            mm1(t, 1)
-            mm1(t, 2)
-        gather(0, 1, relay, XL, XL + 4 * C)
-        gather_tile(1, 2, relay, XL + 5 * C, XL + 5 * C + 4 * P)
-        gather_tile(2, 2, keep)
-        gelu(0)
-        turn_over(0, (0, 1))
-        quant_h(0, relay, HW)
-        gather_tile(1, 3, relay, 0, 4 * P)
-        y00 = layer2([(0, 0)], 0)
-        y01 = layer2([(0, 1)], 1)
-        gelu(1)
-        y02 = layer2([(0, 2)], 2)
-        gather_tile(2, 3, relay, HW + 192, HW + 64)
-        scatter_gated(0, carry(0, y00))
-        z01 = carry(1, y01)
-        turn_over(1, (0, 1))
-        quant_h(1, relay, PL + 64 - H)
-        scatter_gated(1, z01)
-        weigh([(0, 2)], y02, relay, HG)
-        scatter("v", 0, 1, 2)
-        layer1(2, (0, 1, 2))
-        gelu(2)
-        turn_over(2, (4, 5))
-        layer1(3, (2, 0, 1))
-        second = [(1, m) for m in range(NB)]
-        y1 = layer2(second, 4)
-        quant_h(2, keep)
-        weigh(second[:1], y1[:, 0:1, :], relay, 2 * HG)
-        scatter("v", 1, 2, 0)
-        gelu(3)
-        third = [(2, m) for m in range(NB)]
-        turn_over(3, (6, 7))
-        y2 = layer2(third, 6)
-        weigh(second[1:], y1[:, 1:NB, :], relay, S * HG)
-        scatter("s", 1, 2, 2)
-        scatter("s", 1, 2, 1)
-        quant_h(3, keep)
-        weigh(third, y2, relay, 3 * HG)
-        scatter("v", 2, 3, 0)
-        fourth = [(3, m) for m in range(NB)]
-        y3 = layer2(fourth, 3)
-        weigh(fourth, y3, keep)
-        scatter("s", 2, 3, 2)
-        scatter("v", 3, 4, 0)
-        scatter("s", 3, 4, 2)
-        scatter("s", 2, 3, 1)
-        scatter("s", 3, 4, 1)
-        finish(0)
-        finish(2)
-        finish(1, 0, 384)
-        finish(1, 384, T)
+            for b in range(HP):
+                layer1(t, b, (2,))
+        gelu(0, 0, keep)
+        gelu(0, 1, keep)
+        turn_over("v", 0, 0, 0)
+        quant_h(0, 0, 1)
+        turn_over("v", 0, 1, 1)
+        quant_h(0, 1, 2)
+        layer1(2, 0)
+        layer1(2, 1)
+        layer1(3, 0)
+        layer2([(0, 0)], 0)
+        weigh(0, (0,), keep)
+        layer2([(0, 1), (0, 2)], 1)
+        gelu(1, 0, keep)
+        gelu(1, 1, keep)
+        turn_over("v", 1, 0, 2)
+        turn_over("v", 1, 1, 3)
+        quant_h(1)
+        weigh(0, (1, 2), keep)
+        layer1(3, 1)
+        gelu(2, 0, keep)
+        gelu(2, 1, keep)
+        gelu(3, 0, keep)
+        gelu(3, 1, relay, LAST_H)
+        scatter("v", 0, 0)
+        scatter("v", 0, 1)
+        turn_over("s", 2, 0, 4)
+        turn_over("s", 2, 1, 5)
+        turn_over("s", 3, 0, 6)
+        turn_over("s", 3, 1, 7)
+        layer2([(1, 2), (1, 1), (1, 0)], 6)
+        weigh(1, (2, 1, 0), keep)
+        quant_h(2)
+        quant_h(3)
+        win.append(relay.tile([P, T], F32, name="win_last", offset=LAST_H))
+        nc.gpsimd.memset(win[2][:], 0.0)
+        layer2([(2, m) for m in range(NB)], 7)
+        layer2([(3, m) for m in range(NB)], 4)
+        scatter("s", 0, 2)
+        scatter("s", 1, 1)
+        scatter("s", 1, 2)
+        weigh(2, (0, 1, 2), keep)
+        weigh(3, (0, 1, 2), keep)
+        scatter("v", 1, 0)
+        scatter("v", 2, 0)
+        scatter("v", 3, 0)
+        scatter("s", 2, 1)
+        scatter("s", 2, 2)
+        scatter("s", 3, 1)
+        finish(nc.vector, 0)
+        scatter("s", 3, 2)
+        finish(nc.vector, 1)
+        finish(nc.vector, 2, 0, 384)
+        finish(nc.vector, 2, 384, T)

@@ -26,8 +26,8 @@ S = E * C // P
 BANK = 2048
 ROUNDED = 8 * P
 HG = 2 * H
-ROW13 = 10 * ROUNDED
-LAST_H = S * HG
+ROWS12 = 17 * ROUNDED
+X_LOADS = tuple((s, j, j + 1) for s in range(KP) for j in range(4))
 
 
 def tile_moe_res_mlp_gelu_kernel(
@@ -41,13 +41,12 @@ def tile_moe_res_mlp_gelu_kernel(
         relay = ctx.enter_context(tc.tile_pool(name="relay", bufs=1))
 
         offsets = keep.tile([P, E * C // 16], U16, name="offsets")
-        x_row = {
-            (s, j): keep.tile([P, T], F32, align_bytes=64, name="x%d_%d" % (s, j))
-            for s in range(KP)
-            for j in range(4)
-            if (s, j) != (1, 3)
-        }
-        x_row[1, 3] = stage.tile([P, T], F32, align_bytes=64, name="x1_3", offset=ROW13)
+        x_tiles, x_row = {}, {}
+        for s, j0, j1 in X_LOADS:
+            pool, place = (stage, ROWS12) if (s, j0) == (1, 3) else (keep, None)
+            x_tiles[s, j0] = pool.tile([P, j1 - j0, T], F32, align_bytes=64, name="x%d_%d" % (s, j0), offset=place)
+            for j in range(j0, j1):
+                x_row[s, j] = x_tiles[s, j0][:, j - j0, :]
         picked = {
             (s, e): keep.tile([P, 4, C], F32, align_bytes=64, name="picked%d_%d" % (s, e))
             for s in range(KP)
@@ -61,12 +60,17 @@ def tile_moe_res_mlp_gelu_kernel(
             for b in range(HP):
                 w1_t[0, s, b] = w1_by_pass[s][:, b, :]
                 w1_t[1, s, b] = w1_by_half[b][:, s, :]
-        w1_s = [keep.tile([P, KP * H], U8, align_bytes=64, name="w1s_%d" % e) for e in range(E)]
+        early_s = keep.tile([P, 1, H], U8, align_bytes=64, name="w1s_early")
+        late_s = keep.tile([P, 2, H], U8, align_bytes=64, name="w1s_late")
+        other_s = keep.tile([P, KP, H], U8, align_bytes=64, name="w1s_other")
+        w1_s = {(0, 1): early_s[:, 0, :], (0, 0): late_s[:, 0, :], (0, 2): late_s[:, 1, :]}
+        for s in range(KP):
+            w1_s[1, s] = other_s[:, s, :]
         w2_t = [keep.tile([P, HP * 2 * N], U8, align_bytes=64, name="w2_%d" % e) for e in range(E)]
         w2_s = keep.tile([P, E * HP * N], U8, align_bytes=64, name="w2s")
         gate_all = keep.tile([P, E * C], F32, name="gate_all")
         xr_t = keep.tile([P, NB, T], F32, name="xr_t")
-        win = [keep.tile([P, T], F32, name="win_%d" % m) for m in range(NB - 1)]
+        win = [keep.tile([P, T], F32, name="win_%d" % m) for m in range(NB)]
         res = [keep.tile([P, T], F32, name="res_%d" % m) for m in range(NB)]
         h_gr = [relay.tile([P, HP, P, 4], BF16, align_bytes=64, name="h_gr%d" % t, offset=t * HG) for t in range(S)]
         h_words = [keep.tile([P, HP * P], U32, align_bytes=64, name="h_words%d" % t) for t in range(S)]
@@ -76,16 +80,16 @@ def tile_moe_res_mlp_gelu_kernel(
 
         nc.vector.memset(warm[:], 0.0)
         nc.scalar.activation(warm[:], warm[:], ACT.Gelu_apprx_tanh)
-        for tl in w1_s:
+        for tl in (early_s, late_s, other_s):
             nc.vector.memset(tl[:].bitcast(I32), 0)
         nc.vector.memset(w2_s[:].bitcast(I32), 0)
         make_identity(nc, ident[:])
         for tl in win:
             nc.gpsimd.memset(tl[:], 0.0)
 
-        def load_x(s, j):
+        def load_x(s, j0, j1):
             rows = xT[512 * s : 512 * (s + 1), :].rearrange("(p j) w -> p j w", j=4)
-            nc.sync.dma_start(x_row[s, j][:], rows[:, j, :])
+            nc.sync.dma_start(x_tiles[s, j0][:], rows[:, j0:j1, :])
 
         def load_w1_pass(s):
             nc.sync.dma_start(w1_by_pass[s][:].rearrange("p b c -> p (b c)").bitcast(I32), w1_words[0, s].bitcast(I32))
@@ -106,30 +110,27 @@ def tile_moe_res_mlp_gelu_kernel(
             for r in range(4):
                 nc.sync.dma_start(planes[r:P:32], rows[r])
 
-        def load_scales1(e):
-            planes = w1_s[e][:].bitcast(I32).rearrange("p (s c) -> p s c", s=KP)
-            load_scales(planes, w1_scales[e].bitcast(I32).rearrange("s (q r) c -> r q s c", r=4))
+        rows1 = w1_scales.bitcast(I32).rearrange("e s (q r) c -> r q (e s) c", r=4)
 
-        load_x(0, 0)
+        load_x(*X_LOADS[0])
         nc.sync.dma_start(offsets[:], offs)
-        for i in range(1, 8):
-            load_x(i // 4, i % 4)
-        load_scales1(0)
+        for piece in X_LOADS[1:10]:
+            load_x(*piece)
+        load_scales(early_s[:].bitcast(I32), rows1[:, :, 1:2, :])
         load_w1_pass(1)
-        load_x(2, 0)
-        load_x(2, 1)
+        for piece in X_LOADS[10:]:
+            load_x(*piece)
+        load_scales(late_s[:].bitcast(I32), rows1[:, :, 0:KP:2, :])
+        load_w1_pass(0)
+        load_w1_pass(2)
+        load_scales(other_s[:].bitcast(I32), rows1[:, :, KP : E * KP, :])
+        load_w1_half(0)
         load_scales(
             w2_s[:].bitcast(I32).rearrange("p (g c) -> p g c", g=E * HP),
             w2_scales.bitcast(I32).rearrange("e g (q r) c -> r q (e g) c", r=4),
         )
-        load_x(2, 2)
-        load_x(2, 3)
-        load_w1_pass(0)
-        load_scales1(1)
-        load_w1_pass(2)
-        load_w1_half(0)
-        load_w1_half(1)
         load_w2(0)
+        load_w1_half(1)
         nc.sync.dma_start(gate_all[:], gate[0:P, :])
         load_w2(1)
         nc.sync.dma_start(xr_t[:], xr.rearrange("(m p) c -> p m c", p=P))
@@ -137,7 +138,7 @@ def tile_moe_res_mlp_gelu_kernel(
         def gather(eng, s, j, t0, t1):
             e, c0 = t0 // 2, (t0 % 2) * P
             dst = picked[s, e][:, j, c0 : c0 + (t1 - t0) * P]
-            source = x_row[s, j][:].indirect(offsets[:, t0 * P // 16 : t1 * P // 16])
+            source = x_row[s, j].indirect(offsets[:, t0 * P // 16 : t1 * P // 16])
             if eng == "v":
                 nc.vector.tensor_copy(dst, source)
             else:
@@ -148,7 +149,7 @@ def tile_moe_res_mlp_gelu_kernel(
         def gather_rounded(s, j, t0, t1):
             tl = rounded[s, 0][0]
             idx = offsets[:, t0 * P // 16 : t1 * P // 16]
-            nc.vector.tensor_copy(tl[:, t0 * P : t1 * P, j], x_row[s, j][:].indirect(idx))
+            nc.vector.tensor_copy(tl[:, t0 * P : t1 * P, j], x_row[s, j].indirect(idx))
 
         def weave(eng, s, t0, t1, place):
             e, c0, n = t0 // 2, (t0 % 2) * P, (t1 - t0) * P
@@ -187,7 +188,7 @@ def tile_moe_res_mlp_gelu_kernel(
                     lhsT=words.bitcast(FP8X4),
                     lhsT_scale=plane,
                     rhs=w1_t[e, s, b].bitcast(FP4X4),
-                    rhs_scale=w1_s[e][:, s * H + b * 512 : s * H + (b + 1) * 512],
+                    rhs_scale=w1_s[e, s][:, b * 512 : (b + 1) * 512],
                     start=(s == first[e]),
                     stop=(s == KP - 1),
                 )
@@ -237,27 +238,23 @@ def tile_moe_res_mlp_gelu_kernel(
                         stop=(b == HP - 1),
                     )
 
-        gated = {}
+        gated = keep.tile([P, NB, E * C], F32, align_bytes=64, name="gated")
 
-        def weigh(t, blocks, pool, place=None):
-            n = len(blocks)
-            z = pool.tile([P, n, P], F32, align_bytes=64, name="z%d_%d" % (t, blocks[0]), offset=place)
-            factor = gate_all[:, t * P : (t + 1) * P].unsqueeze(1).to_broadcast([P, n, P])
-            sums, i = y[t, blocks[0]]
-            nc.vector.tensor_tensor(z[:], sums[:, i : i + n, :], factor, MULT)
-            for k, m in enumerate(blocks):
-                gated[t, m] = z[:, k, :]
+        def weigh(t, m0, m1):
+            factor = gate_all[:, t * P : (t + 1) * P].unsqueeze(1).to_broadcast([P, m1 - m0, P])
+            sums, i = y[t, m0]
+            nc.vector.tensor_tensor(gated[:, m0:m1, t * P : (t + 1) * P], sums[:, i : i + m1 - m0, :], factor, MULT)
 
-        def scatter(eng, t, m):
-            idx = offsets[:, t * (P // 16) : (t + 1) * (P // 16)]
+        def scatter(eng, m, c0, c1):
+            idx = offsets[:, c0 // 16 : c1 // 16]
             if eng == "v":
-                nc.vector.tensor_copy(win[m][:].indirect(idx), gated[t, m])
+                nc.vector.tensor_copy(win[m][:].indirect(idx), gated[:, m, c0:c1])
             else:
-                nc.scalar.activation(win[m][:].indirect(idx), gated[t, m], ACT.Copy)
+                nc.scalar.activation(win[m][:].indirect(idx), gated[:, m, c0:c1], ACT.Copy)
 
-        def finish(eng, m, c0=0, c1=T):
+        def finish(eng, queue, m, c0=0, c1=T):
             eng.tensor_tensor(res[m][:, c0:c1], win[m][:, c0:c1], xr_t[:, m, c0:c1], ADD)
-            nc.sync.dma_start(out[m * P : (m + 1) * P, c0:c1], res[m][:, c0:c1])
+            queue.dma_start(out[m * P : (m + 1) * P, c0:c1], res[m][:, c0:c1])
 
         for j in range(4):
             gather("v", 0, j, 0, 2)
@@ -267,14 +264,13 @@ def tile_moe_res_mlp_gelu_kernel(
         for j in range(4):
             gather("v", 1, j, 0, 2)
             gather("s", 1, j, 2, 4)
-        weave("v", 1, 0, 2, 13)
-        weave("s", 1, 2, 4, 15)
-        quant_x(0, 0, stage, ROW13)
+        weave("s", 1, 0, 2, 13)
+        quant_x(0, 0, stage, ROWS12)
         quant_x(1, 0, keep)
-        for s in (1, 0):
-            for t in range(2):
-                for b in range(HP):
-                    layer1(t, b, (s,))
+        weave("g", 1, 2, 4, 13)
+        for t in range(2):
+            for b in range(HP):
+                layer1(t, b, (1,))
         last = stage.tile([P, C, 4], BF16, align_bytes=64, name="rounded_last", offset=ROUNDED)
         rounded[2, 0] = (last, 1)
         rounded[2, 1] = (last[:, P:C, :], 2)
@@ -293,57 +289,53 @@ def tile_moe_res_mlp_gelu_kernel(
 
         for t in range(2):
             for b in range(HP):
-                layer1(t, b, (2,))
+                layer1(t, b, (0, 2))
         gelu(0, 0, keep)
         gelu(0, 1, keep)
         turn_over("v", 0, 0, 0)
         quant_h(0, 0, 1)
         turn_over("v", 0, 1, 1)
         quant_h(0, 1, 2)
-        layer1(2, 0)
-        layer1(2, 1)
-        layer1(3, 0)
-        layer2([(0, 0)], 0)
-        weigh(0, (0,), keep)
-        layer2([(0, 1), (0, 2)], 1)
         gelu(1, 0, keep)
         gelu(1, 1, keep)
-        turn_over("v", 1, 0, 2)
-        turn_over("v", 1, 1, 3)
-        quant_h(1)
-        weigh(0, (1, 2), keep)
-        layer1(3, 1)
+        layer1(2, 0)
+        layer1(3, 0)
         gelu(2, 0, keep)
-        gelu(2, 1, keep)
         gelu(3, 0, keep)
-        gelu(3, 1, relay, LAST_H)
-        scatter("v", 0, 0)
-        scatter("v", 0, 1)
-        turn_over("s", 2, 0, 4)
+        layer2([(0, 0)], 0)
+        weigh(0, 0, 1)
+        layer2([(0, 1), (0, 2)], 1)
+        weigh(0, 1, 3)
+        turn_over("s", 1, 0, 0)
+        turn_over("s", 1, 1, 1)
+        quant_h(1)
+        scatter("v", 0, 0, P)
+        scatter("v", 1, 0, P)
+        scatter("v", 2, 0, P)
+        layer1(2, 1)
+        gelu(2, 1, keep)
+        layer1(3, 1)
+        gelu(3, 1, keep)
+        turn_over("s", 2, 0, 0)
         turn_over("s", 2, 1, 5)
-        turn_over("s", 3, 0, 6)
+        turn_over("s", 3, 0, 1)
         turn_over("s", 3, 1, 7)
-        layer2([(1, 2), (1, 1), (1, 0)], 6)
-        weigh(1, (2, 1, 0), keep)
+        layer2([(1, m) for m in range(NB)], 5)
+        weigh(1, 0, 3)
         quant_h(2)
         quant_h(3)
-        win.append(relay.tile([P, T], F32, name="win_last", offset=LAST_H))
-        nc.gpsimd.memset(win[2][:], 0.0)
         layer2([(2, m) for m in range(NB)], 7)
         layer2([(3, m) for m in range(NB)], 4)
-        scatter("s", 0, 2)
-        scatter("s", 1, 1)
-        scatter("s", 1, 2)
-        weigh(2, (0, 1, 2), keep)
-        weigh(3, (0, 1, 2), keep)
-        scatter("v", 1, 0)
-        scatter("v", 2, 0)
-        scatter("v", 3, 0)
-        scatter("s", 2, 1)
-        scatter("s", 2, 2)
-        scatter("s", 3, 1)
-        finish(nc.vector, 0)
-        scatter("s", 3, 2)
-        finish(nc.vector, 1)
-        finish(nc.vector, 2, 0, 384)
-        finish(nc.vector, 2, 384, T)
+        weigh(2, 0, 3)
+        weigh(3, 0, 3)
+        scatter("s", 2, P, 2 * P)
+        scatter("v", 1, P, 2 * P)
+        scatter("s", 2, 2 * P, 4 * P)
+        scatter("v", 0, P, 4 * P)
+        scatter("s", 1, 2 * P, 4 * P)
+        finish(nc.gpsimd, nc.scalar, 2, 0, 384)
+        finish(nc.vector, nc.sync, 2, 384, T)
+        finish(nc.vector, nc.sync, 0, 0, T // 2)
+        finish(nc.vector, nc.sync, 0, T // 2, T)
+        finish(nc.vector, nc.sync, 1, 0, 384)
+        finish(nc.vector, nc.sync, 1, 384, T)

@@ -26,6 +26,7 @@ S = E * C // P
 BANK = 2048
 ROUNDED = 8 * P
 HG = 2 * H
+SPLIT = P + 96
 ROWS12 = 17 * ROUNDED
 X_LOADS = tuple((s, j, j + 1) for s in range(KP) for j in range(4))
 
@@ -114,11 +115,11 @@ def tile_moe_res_mlp_gelu_kernel(
 
         load_x(*X_LOADS[0])
         nc.sync.dma_start(offsets[:], offs)
-        for piece in X_LOADS[1:10]:
+        for piece in X_LOADS[1:9]:
             load_x(*piece)
         load_scales(early_s[:].bitcast(I32), rows1[:, :, 1:2, :])
         load_w1_pass(1)
-        for piece in X_LOADS[10:]:
+        for piece in X_LOADS[9:]:
             load_x(*piece)
         load_scales(late_s[:].bitcast(I32), rows1[:, :, 0:KP:2, :])
         load_w1_pass(0)
@@ -131,8 +132,9 @@ def tile_moe_res_mlp_gelu_kernel(
         )
         load_w2(0)
         load_w1_half(1)
-        nc.sync.dma_start(gate_all[:], gate[0:P, :])
+        nc.sync.dma_start(gate_all[:, 0:C], gate[0:P, 0:C])
         load_w2(1)
+        nc.sync.dma_start(gate_all[:, C : E * C], gate[0:P, C : E * C])
         nc.sync.dma_start(xr_t[:], xr.rearrange("(m p) c -> p m c", p=P))
 
         def gather(eng, s, j, t0, t1):
@@ -329,12 +331,12 @@ def tile_moe_res_mlp_gelu_kernel(
         weigh(2, 0, 3)
         weigh(3, 0, 3)
         scatter("s", 2, P, 2 * P)
-        scatter("v", 1, P, 2 * P)
+        scatter("v", 1, P, SPLIT)
         scatter("s", 2, 2 * P, 4 * P)
         scatter("v", 0, P, 4 * P)
-        scatter("s", 1, 2 * P, 4 * P)
-        finish(nc.gpsimd, nc.scalar, 2, 0, 384)
-        finish(nc.vector, nc.sync, 2, 384, T)
+        scatter("s", 1, SPLIT, 4 * P)
+        finish(nc.gpsimd, nc.scalar, 2, 0, T // 2)
+        finish(nc.vector, nc.sync, 2, T // 2, T)
         finish(nc.vector, nc.sync, 0, 0, T // 2)
         finish(nc.vector, nc.sync, 0, T // 2, T)
         finish(nc.vector, nc.sync, 1, 0, 384)

@@ -26,6 +26,7 @@ S = E * C // P
 BANK = 2048
 ROUNDED = 8 * P
 HG = 2 * H
+OTHER_LOADS = ((0, 2, 0), (2, KP, 0), (0, KP, 1))
 SPLIT = P + 96
 ROWS12 = 17 * ROUNDED
 X_LOADS = tuple((s, j, j + 1) for s in range(KP) for j in range(4))
@@ -55,12 +56,16 @@ def tile_moe_res_mlp_gelu_kernel(
             if (s, e) != (KP - 1, 0)
         }
         w1_by_pass = [keep.tile([P, HP, H], U8, align_bytes=64, name="w1_pass%d" % s) for s in range(KP)]
-        w1_by_half = [keep.tile([P, KP, H], U8, align_bytes=64, name="w1_half%d" % b) for b in range(HP)]
+        w1_other = [
+            keep.tile([P, s1 - s0, H], U8, align_bytes=64, name="w1_other%d_%d" % (s0, b)) for s0, s1, b in OTHER_LOADS
+        ]
         w1_t = {}
         for s in range(KP):
             for b in range(HP):
                 w1_t[0, s, b] = w1_by_pass[s][:, b, :]
-                w1_t[1, s, b] = w1_by_half[b][:, s, :]
+        for tl, (s0, s1, b) in zip(w1_other, OTHER_LOADS):
+            for s in range(s0, s1):
+                w1_t[1, s, b] = tl[:, s - s0, :]
         early_s = keep.tile([P, 1, H], U8, align_bytes=64, name="w1s_early")
         late_s = keep.tile([P, 2, H], U8, align_bytes=64, name="w1s_late")
         other_s = keep.tile([P, KP, H], U8, align_bytes=64, name="w1s_other")
@@ -95,10 +100,11 @@ def tile_moe_res_mlp_gelu_kernel(
         def load_w1_pass(s):
             nc.sync.dma_start(w1_by_pass[s][:].rearrange("p b c -> p (b c)").bitcast(I32), w1_words[0, s].bitcast(I32))
 
-        def load_w1_half(b):
+        def load_w1_other(i):
+            s0, s1, b = OTHER_LOADS[i]
             nc.sync.dma_start(
-                w1_by_half[b][:].bitcast(I32),
-                w1_words[1, :, :, b * H : (b + 1) * H].bitcast(I32).rearrange("s p c -> p s c"),
+                w1_other[i][:].bitcast(I32),
+                w1_words[1, s0:s1, :, b * H : (b + 1) * H].bitcast(I32).rearrange("s p c -> p s c"),
             )
 
         def load_w2(e):
@@ -125,13 +131,14 @@ def tile_moe_res_mlp_gelu_kernel(
         load_w1_pass(0)
         load_w1_pass(2)
         load_scales(other_s[:].bitcast(I32), rows1[:, :, KP : E * KP, :])
-        load_w1_half(0)
         load_scales(
             w2_s[:].bitcast(I32).rearrange("p (g c) -> p g c", g=E * HP),
             w2_scales.bitcast(I32).rearrange("e g (q r) c -> r q (e g) c", r=4),
         )
+        load_w1_other(0)
+        load_w1_other(1)
         load_w2(0)
-        load_w1_half(1)
+        load_w1_other(2)
         nc.sync.dma_start(gate_all[:, 0:C], gate[0:P, 0:C])
         load_w2(1)
         nc.sync.dma_start(gate_all[:, C : E * C], gate[0:P, C : E * C])

@@ -53,7 +53,6 @@ def tile_moe_res_mlp_gelu_kernel(
             (s, e): keep.tile([P, 4, C], F32, align_bytes=64, name="picked%d_%d" % (s, e))
             for s in range(KP)
             for e in range(E)
-            if (s, e) != (KP - 1, 0)
         }
         w1_by_pass = [keep.tile([P, HP, H], U8, align_bytes=64, name="w1_pass%d" % s) for s in range(KP)]
         w1_other = [
@@ -155,10 +154,8 @@ def tile_moe_res_mlp_gelu_kernel(
 
         rounded, codes = {}, {}
 
-        def gather_rounded(s, j, t0, t1):
-            tl = rounded[s, 0][0]
-            idx = offsets[:, t0 * P // 16 : t1 * P // 16]
-            nc.vector.tensor_copy(tl[:, t0 * P : t1 * P, j], x_row[s, j].indirect(idx))
+        def gather_rounded(s, j):
+            nc.vector.tensor_copy(rounded[s, 0][0][:, :, j], x_row[s, j].indirect(offsets[:, 0 : P // 16]))
 
         def weave(eng, s, t0, t1, place):
             e, c0, n = t0 // 2, (t0 % 2) * P, (t1 - t0) * P
@@ -176,10 +173,9 @@ def tile_moe_res_mlp_gelu_kernel(
 
         def quant_x(s, t0, pool, place=None):
             tl, t1 = rounded[s, t0]
-            tl = tl[:, 0 : (t1 - t0) * P, :]
             words = pool.tile([P, (t1 - t0) * P], U32, align_bytes=64, name="x_words%d_%d" % (s, t0), offset=place)
             plane = keep.tile([P, (t1 - t0) * P], U8, align_bytes=64, name="x_bytes%d_%d" % (s, t0))
-            nc.vector.quantize_mx(out=words[:].bitcast(FP8X4), scales=plane[:], in_=tl.rearrange("p c t -> p (c t)"))
+            nc.vector.quantize_mx(out=words[:].bitcast(FP8X4), scales=plane[:], in_=tl[:].rearrange("p c t -> p (c t)"))
             for t in range(t0, t1):
                 codes[s, t] = (words[:, (t - t0) * P : (t - t0 + 1) * P], plane[:, (t - t0) * P : (t - t0 + 1) * P])
 
@@ -280,20 +276,17 @@ def tile_moe_res_mlp_gelu_kernel(
         for t in range(2):
             for b in range(HP):
                 layer1(t, b, (1,))
-        last = stage.tile([P, C, 4], BF16, align_bytes=64, name="rounded_last", offset=ROUNDED)
-        rounded[2, 0] = (last, 1)
-        rounded[2, 1] = (last[:, P:C, :], 2)
-        for j in range(3):
-            gather_rounded(2, j, 0, 2)
+        rounded[2, 0] = (stage.tile([P, P, 4], BF16, align_bytes=64, name="rounded_last", offset=ROUNDED), 1)
+        for j in range(4):
+            gather_rounded(2, j)
+            gather("v", 2, j, 1, 2)
             gather("s", 2, j, 2, 4)
-        gather_rounded(2, 3, 0, 1)
-        gather_rounded(2, 3, 1, 2)
-        gather("s", 2, 3, 2, 4)
         quant_x(2, 0, keep)
+        weave("v", 2, 1, 2, 2)
         quant_x(2, 1, keep)
         weave("s", 2, 2, 4, 3)
-        quant_x(0, 2, stage, ROUNDED // 2)
-        quant_x(1, 2, stage, ROUNDED // 2 + 4 * C)
+        quant_x(0, 2, stage, ROUNDED)
+        quant_x(1, 2, stage, 2 * ROUNDED)
         quant_x(2, 2, keep)
 
         for t in range(2):

@@ -54,21 +54,22 @@ def tile_moe_res_mlp_gelu_kernel(
             for s in range(KP)
             for e in range(E)
         }
-        w1_by_pass = [keep.tile([P, HP, H], U8, align_bytes=64, name="w1_pass%d" % s) for s in range(KP)]
+        w1_early = keep.tile([P, HP, H], U8, align_bytes=64, name="w1_early")
+        w1_late = [keep.tile([P, KP - 1, H], U8, align_bytes=64, name="w1_late%d" % b) for b in range(HP)]
         w1_other = [
             keep.tile([P, s1 - s0, H], U8, align_bytes=64, name="w1_other%d_%d" % (s0, b)) for s0, s1, b in OTHER_LOADS
         ]
         w1_t = {}
         for s in range(KP):
             for b in range(HP):
-                w1_t[0, s, b] = w1_by_pass[s][:, b, :]
+                w1_t[0, s, b] = w1_early[:, b, :] if s == 0 else w1_late[b][:, s - 1, :]
         for tl, (s0, s1, b) in zip(w1_other, OTHER_LOADS):
             for s in range(s0, s1):
                 w1_t[1, s, b] = tl[:, s - s0, :]
         early_s = keep.tile([P, 1, H], U8, align_bytes=64, name="w1s_early")
         late_s = keep.tile([P, 2, H], U8, align_bytes=64, name="w1s_late")
         other_s = keep.tile([P, KP, H], U8, align_bytes=64, name="w1s_other")
-        w1_s = {(0, 1): early_s[:, 0, :], (0, 0): late_s[:, 0, :], (0, 2): late_s[:, 1, :]}
+        w1_s = {(0, 0): early_s[:, 0, :], (0, 1): late_s[:, 0, :], (0, 2): late_s[:, 1, :]}
         for s in range(KP):
             w1_s[1, s] = other_s[:, s, :]
         w2_t = [keep.tile([P, HP * 2 * N], U8, align_bytes=64, name="w2_%d" % e) for e in range(E)]
@@ -96,8 +97,11 @@ def tile_moe_res_mlp_gelu_kernel(
             rows = xT[512 * s : 512 * (s + 1), :].rearrange("(p j) w -> p j w", j=4)
             nc.sync.dma_start(x_tiles[s, j0][:], rows[:, j0:j1, :])
 
-        def load_w1_pass(s):
-            nc.sync.dma_start(w1_by_pass[s][:].rearrange("p b c -> p (b c)").bitcast(I32), w1_words[0, s].bitcast(I32))
+        def load_w1_late(b):
+            nc.sync.dma_start(
+                w1_late[b][:].bitcast(I32),
+                w1_words[0, 1:KP, :, b * H : (b + 1) * H].bitcast(I32).rearrange("s p c -> p s c"),
+            )
 
         def load_w1_other(i):
             s0, s1, b = OTHER_LOADS[i]
@@ -120,15 +124,15 @@ def tile_moe_res_mlp_gelu_kernel(
 
         load_x(*X_LOADS[0])
         nc.sync.dma_start(offsets[:], offs)
-        for piece in X_LOADS[1:9]:
+        for piece in X_LOADS[1:10]:
             load_x(*piece)
-        load_scales(early_s[:].bitcast(I32), rows1[:, :, 1:2, :])
-        load_w1_pass(1)
-        for piece in X_LOADS[9:]:
+        load_scales(early_s[:].bitcast(I32), rows1[:, :, 0:1, :])
+        nc.sync.dma_start(w1_early[:].rearrange("p b c -> p (b c)").bitcast(I32), w1_words[0, 0].bitcast(I32))
+        for piece in X_LOADS[10:]:
             load_x(*piece)
-        load_scales(late_s[:].bitcast(I32), rows1[:, :, 0:KP:2, :])
-        load_w1_pass(0)
-        load_w1_pass(2)
+        load_scales(late_s[:].bitcast(I32), rows1[:, :, 1:KP, :])
+        load_w1_late(0)
+        load_w1_late(1)
         load_scales(other_s[:].bitcast(I32), rows1[:, :, KP : E * KP, :])
         load_scales(
             w2_s[:].bitcast(I32).rearrange("p (g c) -> p g c", g=E * HP),
@@ -180,7 +184,7 @@ def tile_moe_res_mlp_gelu_kernel(
                 codes[s, t] = (words[:, (t - t0) * P : (t - t0 + 1) * P], plane[:, (t - t0) * P : (t - t0 + 1) * P])
 
         banks, h_bf = {}, {}
-        first = (1, 0)
+        first = (0, 0)
 
         def layer1(t, b, passes=range(KP)):
             e = t // 2
@@ -264,18 +268,17 @@ def tile_moe_res_mlp_gelu_kernel(
         for j in range(4):
             gather("v", 0, j, 0, 2)
             gather("s", 0, j, 2, 4)
-        weave("g", 0, 0, 2, 6)
+        weave("s", 0, 0, 2, 6)
         weave("g", 0, 2, 4, 8)
+        quant_x(0, 0, keep)
         for j in range(4):
             gather("v", 1, j, 0, 2)
             gather("s", 1, j, 2, 4)
-        weave("s", 1, 0, 2, 13)
-        quant_x(0, 0, stage, ROWS12)
+        weave("g", 1, 0, 2, 13)
         quant_x(1, 0, keep)
-        weave("g", 1, 2, 4, 13)
         for t in range(2):
             for b in range(HP):
-                layer1(t, b, (1,))
+                layer1(t, b, (0,))
         rounded[2, 0] = (stage.tile([P, P, 4], BF16, align_bytes=64, name="rounded_last", offset=ROUNDED), 1)
         for j in range(4):
             gather_rounded(2, j)
@@ -284,14 +287,15 @@ def tile_moe_res_mlp_gelu_kernel(
         quant_x(2, 0, keep)
         weave("v", 2, 1, 2, 2)
         quant_x(2, 1, keep)
-        weave("s", 2, 2, 4, 3)
+        weave("s", 2, 2, 4, 4)
         quant_x(0, 2, stage, ROUNDED)
-        quant_x(1, 2, stage, 2 * ROUNDED)
+        weave("v", 1, 2, 4, 2)
         quant_x(2, 2, keep)
+        quant_x(1, 2, keep)
 
         for t in range(2):
             for b in range(HP):
-                layer1(t, b, (0, 2))
+                layer1(t, b, (1, 2))
         gelu(0, 0, keep)
         gelu(0, 1, keep)
         turn_over("v", 0, 0, 0)

@@ -28,8 +28,7 @@ ROUNDED = 8 * P
 HG = 2 * H
 OTHER_LOADS = ((0, 2, 0), (2, KP, 0), (0, KP, 1))
 SPLIT = P + 96
-ROWS12 = 17 * ROUNDED
-X_LOADS = tuple((s, j, j + 1) for s in range(KP) for j in range(4))
+X_LOADS = ((0, 0, 2), (0, 2, 4), (1, 0, 2), (1, 2, 4), (2, 0, 2), (2, 2, 3), (2, 3, 4))
 
 
 def tile_moe_res_mlp_gelu_kernel(
@@ -45,8 +44,7 @@ def tile_moe_res_mlp_gelu_kernel(
         offsets = keep.tile([P, E * C // 16], U16, name="offsets")
         x_tiles, x_row = {}, {}
         for s, j0, j1 in X_LOADS:
-            pool, place = (stage, ROWS12) if (s, j0) == (1, 3) else (keep, None)
-            x_tiles[s, j0] = pool.tile([P, j1 - j0, T], F32, align_bytes=64, name="x%d_%d" % (s, j0), offset=place)
+            x_tiles[s, j0] = keep.tile([P, j1 - j0, T], F32, align_bytes=256, name="x%d_%d" % (s, j0))
             for j in range(j0, j1):
                 x_row[s, j] = x_tiles[s, j0][:, j - j0, :]
         picked = {
@@ -124,11 +122,11 @@ def tile_moe_res_mlp_gelu_kernel(
 
         load_x(*X_LOADS[0])
         nc.sync.dma_start(offsets[:], offs)
-        for piece in X_LOADS[1:10]:
+        for piece in X_LOADS[1:5]:
             load_x(*piece)
         load_scales(early_s[:].bitcast(I32), rows1[:, :, 0:1, :])
         nc.sync.dma_start(w1_early[:].rearrange("p b c -> p (b c)").bitcast(I32), w1_words[0, 0].bitcast(I32))
-        for piece in X_LOADS[10:]:
+        for piece in X_LOADS[5:]:
             load_x(*piece)
         load_scales(late_s[:].bitcast(I32), rows1[:, :, 1:KP, :])
         load_w1_late(0)

@@ -72,6 +72,7 @@ def tile_moe_res_mlp_gelu_kernel(
             w1_s[1, s] = other_s[:, s, :]
         w2_t = [keep.tile([P, HP * 2 * N], U8, align_bytes=64, name="w2_%d" % e) for e in range(E)]
         w2_s = keep.tile([P, E * HP * N], U8, align_bytes=64, name="w2s")
+        gate_col = keep.tile([P, 4], F32, name="gate_col")
         gate_all = keep.tile([P, E * C], F32, name="gate_all")
         xr_t = keep.tile([P, NB, T], F32, name="xr_t")
         win = [keep.tile([P, T], F32, name="win_%d" % m) for m in range(NB)]
@@ -82,6 +83,7 @@ def tile_moe_res_mlp_gelu_kernel(
         ident = keep.tile([P, P], F32, name="ident")
         warm = keep.tile([P, 1], F32, name="warm")
 
+        nc.scalar.dma_start(gate_col[:], gate[0:1, :].rearrange("o (p j) -> p (o j)", j=4))
         nc.vector.memset(warm[:], 0.0)
         nc.scalar.activation(warm[:], warm[:], ACT.Gelu_apprx_tanh)
         for tl in (early_s, late_s, other_s):
@@ -140,10 +142,13 @@ def tile_moe_res_mlp_gelu_kernel(
         load_w1_other(1)
         load_w2(0)
         load_w1_other(2)
-        nc.sync.dma_start(gate_all[:, 0:C], gate[0:P, 0:C])
         load_w2(1)
-        nc.sync.dma_start(gate_all[:, C : E * C], gate[0:P, C : E * C])
         nc.sync.dma_start(xr_t[:], xr.rearrange("(m p) c -> p m c", p=P))
+
+        spread = turn.tile([P, 4, P], F32, name="spread", offset=BANK * 7)
+        for j in range(4):
+            nc.tensor.transpose(spread[:, j, :], gate_col[:, j : j + 1].to_broadcast([P, P]), ident[:])
+        nc.vector.tensor_copy(gate_all[:].rearrange("p (n j) -> p n j", j=4), spread[:].rearrange("p j n -> p n j"))
 
         def gather(eng, s, j, t0, t1):
             e, c0 = t0 // 2, (t0 % 2) * P
@@ -208,16 +213,18 @@ def tile_moe_res_mlp_gelu_kernel(
                 ACT.Gelu_apprx_tanh,
             )
 
-        def turn_over(eng, t, b, bank):
-            xt = turn.tile([P, 2, P], F32, name="xt%d_%d" % (t, b), offset=BANK * bank)
-            pairs = h_bf[t, b][:].bitcast(F32)
-            for u in range(2):
-                nc.tensor.transpose(xt[:, u, :], pairs[:, u * P : (u + 1) * P], ident[:])
-            dst = h_gr[t][:, b].rearrange("p c t -> p (c t)").bitcast(F32).rearrange("p (c u) -> p c u", u=2)
+        def turn_over(eng, t, b0, bank, halves=1):
+            xt = turn.tile([P, halves, 2, P], F32, name="xt%d_%d" % (t, b0), offset=BANK * bank)
+            for b in range(halves):
+                pairs = h_bf[t, b0 + b][:].bitcast(F32)
+                for u in range(2):
+                    nc.tensor.transpose(xt[:, b, u, :], pairs[:, u * P : (u + 1) * P], ident[:])
+            words = h_gr[t][:, b0 : b0 + halves].rearrange("p b c t -> p b (c t)").bitcast(F32)
+            dst = words.rearrange("p b (c u) -> p b c u", u=2)
             if eng == "v":
-                nc.vector.tensor_copy(dst, xt[:].rearrange("p u c -> p c u"))
+                nc.vector.tensor_copy(dst, xt[:].rearrange("p b u c -> p b c u"))
             else:
-                nc.scalar.copy(dst, xt[:].rearrange("p u c -> p c u"))
+                nc.scalar.copy(dst, xt[:].rearrange("p b u c -> p b c u"))
 
         def quant_h(t, b0=0, b1=HP):
             nc.vector.quantize_mx(
@@ -310,8 +317,7 @@ def tile_moe_res_mlp_gelu_kernel(
         weigh(0, 0, 1)
         layer2([(0, 1), (0, 2)], 1)
         weigh(0, 1, 3)
-        turn_over("s", 1, 0, 0)
-        turn_over("s", 1, 1, 1)
+        turn_over("s", 1, 0, 0, HP)
         quant_h(1)
         scatter("v", 0, 0, P)
         scatter("v", 1, 0, P)

from contextlib import ExitStack

import concourse.mybir as mybir
from concourse.masks import make_identity

K, T, E, C, H, N = 1536, 640, 2, 256, 1024, 384
P = 128
FLOPS = 2 * E * C * (K * H + H * N)

F32 = mybir.dt.float32
BF16 = mybir.dt.bfloat16
I32 = mybir.dt.int32
U32 = mybir.dt.uint32
U16 = mybir.dt.uint16
U8 = mybir.dt.uint8
FP8X4 = mybir.dt.float8_e4m3fn_x4
FP4X4 = mybir.dt.float4_e2m1fn_x4
ACT = mybir.ActivationFunctionType
MULT = mybir.AluOpType.mult
ADD = mybir.AluOpType.add

KP = K // 512
HP = H // 512
NB = N // P
S = E * C // P
BANK = 2048
ROUNDED = 8 * P
HG = 2 * H
OTHER_LOADS = ((0, 2, 0), (2, KP, 0), (0, KP, 1))
SPLIT = P + 96
X_LOADS = ((0, 0, 2), (0, 2, 4), (1, 0, 2), (1, 2, 4), (2, 0, 2), (2, 2, 3), (2, 3, 4))


def tile_moe_res_mlp_gelu_kernel(
    tc, xT, xr, w1_words, w1_scales, w2_words, w2_scales, gate, offs, out
):
    nc = tc.nc
    with ExitStack() as ctx:
        keep = ctx.enter_context(tc.tile_pool(name="keep", bufs=1))
        turn = ctx.enter_context(tc.psum_pool(name="turn", bufs=1))
        stage = ctx.enter_context(tc.tile_pool(name="stage", bufs=1))
        relay = ctx.enter_context(tc.tile_pool(name="relay", bufs=1))

        offsets = keep.tile([P, E * C // 16], U16, name="offsets")
        x_tiles, x_row = {}, {}
        for s, j0, j1 in X_LOADS:
            x_tiles[s, j0] = keep.tile([P, j1 - j0, T], F32, align_bytes=256, name="x%d_%d" % (s, j0))
            for j in range(j0, j1):
                x_row[s, j] = x_tiles[s, j0][:, j - j0, :]
        picked = {
            (s, e): keep.tile([P, 4, C], F32, align_bytes=64, name="picked%d_%d" % (s, e))
            for s in range(KP)
            for e in range(E)
        }
        w1_early = keep.tile([P, HP, H], U8, align_bytes=64, name="w1_early")
        w1_late = [keep.tile([P, KP - 1, H], U8, align_bytes=64, name="w1_late%d" % b) for b in range(HP)]
        w1_other = [
            keep.tile([P, s1 - s0, H], U8, align_bytes=64, name="w1_other%d_%d" % (s0, b)) for s0, s1, b in OTHER_LOADS
        ]
        w1_t = {}
        for s in range(KP):
            for b in range(HP):
                w1_t[0, s, b] = w1_early[:, b, :] if s == 0 else w1_late[b][:, s - 1, :]
        for tl, (s0, s1, b) in zip(w1_other, OTHER_LOADS):
            for s in range(s0, s1):
                w1_t[1, s, b] = tl[:, s - s0, :]
        early_s = keep.tile([P, 1, H], U8, align_bytes=64, name="w1s_early")
        late_s = keep.tile([P, 2, H], U8, align_bytes=64, name="w1s_late")
        other_s = keep.tile([P, KP, H], U8, align_bytes=64, name="w1s_other")
        w1_s = {(0, 0): early_s[:, 0, :], (0, 1): late_s[:, 0, :], (0, 2): late_s[:, 1, :]}
        for s in range(KP):
            w1_s[1, s] = other_s[:, s, :]
        w2_t = [keep.tile([P, HP * 2 * N], U8, align_bytes=64, name="w2_%d" % e) for e in range(E)]
        w2_s = keep.tile([P, E * HP * N], U8, align_bytes=64, name="w2s")
        gate_col = keep.tile([P, 4], F32, name="gate_col")
        gate_all = keep.tile([P, E * C], F32, name="gate_all")
        xr_t = keep.tile([P, NB, T], F32, name="xr_t")
        win = [keep.tile([P, T], F32, name="win_%d" % m) for m in range(NB)]
        res = [keep.tile([P, T], F32, name="res_%d" % m) for m in range(NB)]
        h_gr = [relay.tile([P, HP, P, 4], BF16, align_bytes=64, name="h_gr%d" % t, offset=t * HG) for t in range(S)]
        h_words = [keep.tile([P, HP * P], U32, align_bytes=64, name="h_words%d" % t) for t in range(S)]
        h_bytes = [keep.tile([P, HP * P], U8, align_bytes=64, name="h_bytes%d" % t) for t in range(S)]
        ident = keep.tile([P, P], F32, name="ident")
        warm = keep.tile([P, 1], F32, name="warm")

        nc.scalar.dma_start(gate_col[:], gate[0:1, :].rearrange("o (p j) -> p (o j)", j=4))
        nc.vector.memset(warm[:], 0.0)
        nc.scalar.activation(warm[:], warm[:], ACT.Gelu_apprx_tanh)
        for tl in (early_s, late_s, other_s):
            nc.vector.memset(tl[:].bitcast(I32), 0)
        nc.vector.memset(w2_s[:].bitcast(I32), 0)
        make_identity(nc, ident[:])
        for tl in win:
            nc.gpsimd.memset(tl[:], 0.0)

        def load_x(s, j0, j1):
            rows = xT[512 * s : 512 * (s + 1), :].rearrange("(p j) w -> p j w", j=4)
            nc.sync.dma_start(x_tiles[s, j0][:], rows[:, j0:j1, :])

        def load_w1_late(b):
            nc.sync.dma_start(
                w1_late[b][:].bitcast(I32),
                w1_words[0, 1:KP, :, b * H : (b + 1) * H].bitcast(I32).rearrange("s p c -> p s c"),
            )

        def load_w1_other(i):
            s0, s1, b = OTHER_LOADS[i]
            nc.sync.dma_start(
                w1_other[i][:].bitcast(I32),
                w1_words[1, s0:s1, :, b * H : (b + 1) * H].bitcast(I32).rearrange("s p c -> p s c"),
            )

        def load_w2(e):
            nc.sync.dma_start(
                w2_t[e][:].bitcast(I32).rearrange("p (g c) -> p g c", g=HP),
                w2_words[e].bitcast(I32).rearrange("g p c -> p g c"),
            )

        def load_scales(planes, rows):
            for r in range(4):
                nc.sync.dma_start(planes[r:P:32], rows[r])

        rows1 = w1_scales.bitcast(I32).rearrange("e s (q r) c -> r q (e s) c", r=4)

        load_x(*X_LOADS[0])
        nc.sync.dma_start(offsets[:], offs)
        for piece in X_LOADS[1:5]:
            load_x(*piece)
        load_scales(early_s[:].bitcast(I32), rows1[:, :, 0:1, :])
        nc.sync.dma_start(w1_early[:].rearrange("p b c -> p (b c)").bitcast(I32), w1_words[0, 0].bitcast(I32))
        for piece in X_LOADS[5:]:
            load_x(*piece)
        load_scales(late_s[:].bitcast(I32), rows1[:, :, 1:KP, :])
        load_w1_late(0)
        load_w1_late(1)
        load_scales(other_s[:].bitcast(I32), rows1[:, :, KP : E * KP, :])
        load_scales(
            w2_s[:].bitcast(I32).rearrange("p (g c) -> p g c", g=E * HP),
            w2_scales.bitcast(I32).rearrange("e g (q r) c -> r q (e g) c", r=4),
        )
        load_w1_other(0)
        load_w1_other(1)
        load_w2(0)
        load_w1_other(2)
        load_w2(1)
        nc.sync.dma_start(xr_t[:], xr.rearrange("(m p) c -> p m c", p=P))

        spread = turn.tile([P, 4, P], F32, name="spread", offset=BANK * 7)
        for j in range(4):
            nc.tensor.transpose(spread[:, j, :], gate_col[:, j : j + 1].to_broadcast([P, P]), ident[:])
        nc.vector.tensor_copy(gate_all[:].rearrange("p (n j) -> p n j", j=4), spread[:].rearrange("p j n -> p n j"))

        def gather(eng, s, j, t0, t1):
            e, c0 = t0 // 2, (t0 % 2) * P
            dst = picked[s, e][:, j, c0 : c0 + (t1 - t0) * P]
            source = x_row[s, j].indirect(offsets[:, t0 * P // 16 : t1 * P // 16])
            if eng == "v":
                nc.vector.tensor_copy(dst, source)
            else:
                nc.scalar.activation(dst, source, ACT.Copy)

        rounded, codes = {}, {}

        def gather_rounded(s, j):
            nc.vector.tensor_copy(rounded[s, 0][0][:, :, j], x_row[s, j].indirect(offsets[:, 0 : P // 16]))

        def weave(eng, s, t0, t1, place):
            e, c0, n = t0 // 2, (t0 % 2) * P, (t1 - t0) * P
            tl = stage.tile([P, n, 4], BF16, align_bytes=64, name="rounded%d_%d" % (s, t0), offset=place * ROUNDED)
            source = picked[s, e][:, :, c0 : c0 + n]
            if eng == "g":
                nc.gpsimd.tensor_copy(tl[:], source.rearrange("p t c -> p c t"))
            else:
                dst, source = tl[:].rearrange("p (c i) t -> p c t i", i=4), source.rearrange("p t (c i) -> p c t i", i=4)
                if eng == "v":
                    nc.vector.tensor_copy(dst, source)
                else:
                    nc.scalar.activation(dst, source, ACT.Copy)
            rounded[s, t0] = (tl, t1)

        def quant_x(s, t0, pool, place=None):
            tl, t1 = rounded[s, t0]
            words = pool.tile([P, (t1 - t0) * P], U32, align_bytes=64, name="x_words%d_%d" % (s, t0), offset=place)
            plane = keep.tile([P, (t1 - t0) * P], U8, align_bytes=64, name="x_bytes%d_%d" % (s, t0))
            nc.vector.quantize_mx(out=words[:].bitcast(FP8X4), scales=plane[:], in_=tl[:].rearrange("p c t -> p (c t)"))
            for t in range(t0, t1):
                codes[s, t] = (words[:, (t - t0) * P : (t - t0 + 1) * P], plane[:, (t - t0) * P : (t - t0 + 1) * P])

        banks, h_bf = {}, {}
        first = (0, 0)

        def layer1(t, b, passes=range(KP)):
            e = t // 2
            for s in passes:
                if s == first[e]:
                    banks[t, b] = turn.tile([P, 512], F32, name="acc%d_%d" % (t, b), offset=BANK * (2 * t + b))
                words, plane = codes[s, t]
                nc.tensor.matmul_mx(
                    out=banks[t, b][:],
                    lhsT=words.bitcast(FP8X4),
                    lhsT_scale=plane,
                    rhs=w1_t[e, s, b].bitcast(FP4X4),
                    rhs_scale=w1_s[e, s][:, b * 512 : (b + 1) * 512],
                    start=(s == first[e]),
                    stop=(s == KP - 1),
                )

        def gelu(t, b, pool, place=None):
            h_bf[t, b] = pool.tile([P, 512], BF16, align_bytes=64, name="h_bf%d_%d" % (t, b), offset=place)
            nc.scalar.activation(
                h_bf[t, b][:].rearrange("c (u p e) -> c u p e", u=2, e=2),
                banks[t, b][:].rearrange("c (p u e) -> c u p e", u=2, e=2),
                ACT.Gelu_apprx_tanh,
            )

        def turn_over(eng, t, b0, bank, halves=1):
            xt = turn.tile([P, halves, 2, P], F32, name="xt%d_%d" % (t, b0), offset=BANK * bank)
            for b in range(halves):
                pairs = h_bf[t, b0 + b][:].bitcast(F32)
                for u in range(2):
                    nc.tensor.transpose(xt[:, b, u, :], pairs[:, u * P : (u + 1) * P], ident[:])
            words = h_gr[t][:, b0 : b0 + halves].rearrange("p b c t -> p b (c t)").bitcast(F32)
            dst = words.rearrange("p b (c u) -> p b c u", u=2)
            if eng == "v":
                nc.vector.tensor_copy(dst, xt[:].rearrange("p b u c -> p b c u"))
            else:
                nc.scalar.copy(dst, xt[:].rearrange("p b u c -> p b c u"))

        def quant_h(t, b0=0, b1=HP):
            nc.vector.quantize_mx(
                out=h_words[t][:, b0 * P : b1 * P].bitcast(FP8X4),
                scales=h_bytes[t][:, b0 * P : b1 * P],
                in_=h_gr[t][:, b0:b1].rearrange("p b c t -> p (b c t)"),
            )

        y = {}

        def layer2(items, bank):
            sums = turn.tile([P, len(items), P], F32, name="y%d_%d" % items[0], offset=BANK * bank)
            for i, (t, m) in enumerate(items):
                e = t // 2
                y[t, m] = (sums, i)
                for b in range(HP):
                    w0 = b * N + m * P
                    nc.tensor.matmul_mx(
                        out=sums[:, i, :],
                        lhsT=w2_t[e][:, 2 * w0 : 2 * (w0 + P)].bitcast(FP4X4),
                        lhsT_scale=w2_s[:, e * HP * N + w0 : e * HP * N + w0 + P],
                        rhs=h_words[t][:, b * P : (b + 1) * P].bitcast(FP8X4),
                        rhs_scale=h_bytes[t][:, b * P : (b + 1) * P],
                        start=(b == 0),
                        stop=(b == HP - 1),
                    )

        gated = keep.tile([P, NB, E * C], F32, align_bytes=64, name="gated")

        def weigh(t, m0, m1):
            factor = gate_all[:, t * P : (t + 1) * P].unsqueeze(1).to_broadcast([P, m1 - m0, P])
            sums, i = y[t, m0]
            nc.vector.tensor_tensor(gated[:, m0:m1, t * P : (t + 1) * P], sums[:, i : i + m1 - m0, :], factor, MULT)

        def scatter(eng, m, c0, c1):
            idx = offsets[:, c0 // 16 : c1 // 16]
            if eng == "v":
                nc.vector.tensor_copy(win[m][:].indirect(idx), gated[:, m, c0:c1])
            else:
                nc.scalar.activation(win[m][:].indirect(idx), gated[:, m, c0:c1], ACT.Copy)

        def finish(eng, queue, m, c0=0, c1=T):
            eng.tensor_tensor(res[m][:, c0:c1], win[m][:, c0:c1], xr_t[:, m, c0:c1], ADD)
            queue.dma_start(out[m * P : (m + 1) * P, c0:c1], res[m][:, c0:c1])

        for j in range(4):
            gather("v", 0, j, 0, 2)
            gather("s", 0, j, 2, 4)
        weave("s", 0, 0, 2, 6)
        weave("g", 0, 2, 4, 8)
        quant_x(0, 0, keep)
        for j in range(4):
            gather("v", 1, j, 0, 2)
            gather("s", 1, j, 2, 4)
        weave("g", 1, 0, 2, 13)
        quant_x(1, 0, keep)
        for t in range(2):
            for b in range(HP):
                layer1(t, b, (0,))
        rounded[2, 0] = (stage.tile([P, P, 4], BF16, align_bytes=64, name="rounded_last", offset=ROUNDED), 1)
        for j in range(4):
            gather_rounded(2, j)
            gather("v", 2, j, 1, 2)
            gather("s", 2, j, 2, 4)
        quant_x(2, 0, keep)
        weave("v", 2, 1, 2, 2)
        quant_x(2, 1, keep)
        weave("s", 2, 2, 4, 4)
        quant_x(0, 2, stage, ROUNDED)
        weave("v", 1, 2, 4, 2)
        quant_x(2, 2, keep)
        quant_x(1, 2, keep)

        for t in range(2):
            for b in range(HP):
                layer1(t, b, (1, 2))
        gelu(0, 0, keep)
        gelu(0, 1, keep)
        turn_over("v", 0, 0, 0)
        quant_h(0, 0, 1)
        turn_over("v", 0, 1, 1)
        quant_h(0, 1, 2)
        gelu(1, 0, keep)
        gelu(1, 1, keep)
        layer1(2, 0)
        layer1(3, 0)
        gelu(2, 0, keep)
        gelu(3, 0, keep)
        layer2([(0, 0)], 0)
        weigh(0, 0, 1)
        layer2([(0, 1), (0, 2)], 1)
        weigh(0, 1, 3)
        turn_over("s", 1, 0, 0, HP)
        quant_h(1)
        scatter("v", 0, 0, P)
        scatter("v", 1, 0, P)
        scatter("v", 2, 0, P)
        layer1(2, 1)
        gelu(2, 1, keep)
        layer1(3, 1)
        gelu(3, 1, keep)
        turn_over("s", 2, 0, 0)
        turn_over("s", 2, 1, 5)
        turn_over("s", 3, 0, 1)
        turn_over("s", 3, 1, 7)
        layer2([(1, m) for m in range(NB)], 5)
        weigh(1, 0, 3)
        quant_h(2)
        quant_h(3)
        layer2([(2, m) for m in range(NB)], 7)
        layer2([(3, m) for m in range(NB)], 4)
        weigh(2, 0, 3)
        weigh(3, 0, 3)
        scatter("s", 2, P, 2 * P)
        scatter("v", 1, P, SPLIT)
        scatter("s", 2, 2 * P, 4 * P)
        scatter("v", 0, P, 4 * P)
        scatter("s", 1, SPLIT, 4 * P)
        finish(nc.gpsimd, nc.scalar, 2, 0, T // 2)
        finish(nc.vector, nc.sync, 2, T // 2, T)
        finish(nc.vector, nc.sync, 0, 0, T // 2)
        finish(nc.vector, nc.sync, 0, T // 2, T)
        finish(nc.vector, nc.sync, 1, 0, 384)
        finish(nc.vector, nc.sync, 1, 384, T)
